import numpy as np
import ml_dtypes


def mxq(x, axis, fmt="e4m3"):
    dtype, down = {"e4m3": (ml_dtypes.float8_e4m3fn, 7), "e5m2": (ml_dtypes.float8_e5m2, 14)}[fmt]
    v = np.moveaxis(np.asarray(x, np.float32).astype(ml_dtypes.bfloat16).astype(np.float64), axis, -1)
    blocks = v.reshape(v.shape[:-1] + (-1, 32))
    amax = np.abs(blocks).max(-1, keepdims=True)
    byte = np.maximum(np.where(amax > 0, np.frexp(amax)[1] - 1 + 127, 0) - down, 1)
    scale = np.exp2(byte - 127.0)
    codes = (blocks / scale).astype(np.float32).astype(dtype).astype(np.float64)
    return np.moveaxis((codes * scale).reshape(v.shape), -1, axis)


WIDE = False


def mx_kscale(k):
    if not WIDE:
        return np.ones(k)
    levels = np.array([24, -24, 12, -12, 0])
    if k % 512:
        return np.exp2(np.random.permutation(np.resize(levels, k // 32))).repeat(32)
    a = np.empty((k // 512, 16))
    for p in range(k // 512):
        a[p, :8] = np.random.permutation(np.resize(levels, 8))
        for g in range(8):
            far = levels[np.abs(levels - a[p, g]) >= 10]
            a[p, g + 8] = far[np.random.randint(len(far))]
    return np.exp2(a.ravel()).repeat(32)


def f64(x):
    return np.asarray(x).astype(np.float64)


def striped(idx):
    return np.tile(idx.reshape(-1, 16).T, (8, 1)).astype(np.uint16)


def unstriped(offs):
    return offs[:16].T.reshape(-1).astype(np.int64)


E2M1 = np.array([0.0, 0.5, 1.0, 1.5, 2.0, 3.0, 4.0, 6.0, -0.0, -0.5, -1.0, -1.5, -2.0, -3.0, -4.0, -6.0])


def pack_weight(w, fmt):
    k, n = w.shape
    w = f64(np.asarray(w, np.float32).astype(ml_dtypes.bfloat16)).reshape(k // 32, 32, n)
    amax = np.abs(w).max(1)
    if fmt == "e4m3":
        byte = np.frexp(amax)[1] - 1 + 127 - 7
    else:
        mant, ex = np.frexp(amax / 6.0)
        byte = np.where(mant > 0.5, ex, ex - 1) + 127
    byte = np.clip(np.where(amax > 0, byte, 1), 1, 254)
    scaled = (w * np.exp2(127.0 - byte)[:, None, :]).reshape(k, n).astype(np.float32)
    by_word = np.ascontiguousarray(scaled.reshape(k // 512, 128, 4, n).transpose(0, 1, 3, 2))
    if fmt == "e4m3":
        words = by_word.astype(ml_dtypes.float8_e4m3fn).view(np.uint8)
    else:
        c = by_word.astype(ml_dtypes.float4_e2m1fn).view(np.uint8) & 0xF
        words = (c[..., 0::2] | (c[..., 1::2] << 4)).reshape(k // 512, 128, 2 * n)
    return np.ascontiguousarray(words), np.ascontiguousarray(byte.astype(np.uint8).reshape(k // 512, 16, n))


def unpack_weight(words, scales, fmt):
    g, _, n = scales.shape
    words = np.ascontiguousarray(words).reshape(g, 128, n, -1)
    if fmt == "e4m3":
        vals = words.view(ml_dtypes.float8_e4m3fn).astype(np.float64)
    else:
        nib = np.empty((g, 128, n, 4), np.uint8)
        nib[..., 0::2] = words & 0xF
        nib[..., 1::2] = words >> 4
        vals = E2M1[nib]
    vals = vals * np.repeat(np.exp2(scales.astype(np.float64) - 127.0), 8, axis=1)[..., None]
    return vals.transpose(0, 1, 3, 2).reshape(g * 512, n)


K, L, N, T, J = 1024, 1024, 512, 2048, 1024


def setup_inputs():
    n = np.random.standard_normal
    s = mx_kscale(K)[:, None]
    s2 = mx_kscale(L)[:, None]
    p_tab = pack_weight(n((K, T)) * s, "e4m3")
    p_wx = pack_weight(n((L, N)) / np.sqrt(L) / s2, "e4m3")
    return {
        "tab_words": p_tab[0],
        "tab_scales": p_tab[1],
        "wt": (n((K, N)) / np.sqrt(K) / s).astype(np.float32),
        "x": (n((L, J)) * s2).astype(np.float32),
        "wx_words": p_wx[0],
        "wx_scales": p_wx[1],
        "b": (0.3 * n(N)).astype(np.float32),
        "offs": striped(np.random.permutation(T)[:J]),
    }


def reference(tab_words, tab_scales, wt, x, wx_words, wx_scales, b, offs):
    idx = unstriped(offs)
    tab_ = unpack_weight(tab_words, tab_scales, "e4m3")[:, idx]
    wt_q_ = mxq(f64(wt), 0, "e4m3")
    wt_r_ = mxq(f64(wt) - wt_q_, 0, "e4m3")
    x_ = mxq(f64(x), 0, "e4m3")
    wx_ = unpack_weight(wx_words, wx_scales, "e4m3")
    y = wt_q_.T @ tab_ + wt_r_.T @ tab_ + wx_.T @ x_
    return y + f64(b)[:, None]

@@ -1,0 +1,294 @@
+from contextlib import ExitStack
+
+import concourse.mybir as mybir
+from concourse.masks import make_identity
+
+K, L, N, T, J = 1024, 1024, 512, 2048, 1024
+FLOPS = 3758096384
+
+F32 = mybir.dt.float32
+BF16 = mybir.dt.bfloat16
+I32 = mybir.dt.int32
+U32 = mybir.dt.uint32
+U16 = mybir.dt.uint16
+U8 = mybir.dt.uint8
+FP8X4 = mybir.dt.float8_e4m3fn_x4
+IDENTITY = mybir.ActivationFunctionType.Identity
+SUBTRACT = mybir.AluOpType.subtract
+ADD = mybir.AluOpType.add
+
+P = 128
+PACK = 4
+K_PASS = P * PACK
+PASSES = K // K_PASS
+N_TILES = N // P
+HALF = J // 2
+QUARTER = J // 4
+RUN = 4
+
+
+def tile_list_tiert_bias_kernel(
+    tc, tab_words, tab_scales, wt, x, wx_words, wx_scales, b, offs, out
+):
+    nc = tc.nc
+    with ExitStack() as ctx:
+        sb = ctx.enter_context(tc.tile_pool(name="sb", bufs=1))
+        psum = ctx.enter_context(tc.psum_pool(name="psum", bufs=1))
+
+        def tile(shape, dtype, name, slot=None):
+            return sb.tile(shape, dtype, name=name, tag=slot or name, align_bytes=64)
+
+        offsets = sb.tile([P, J // 16], U16, name="offsets")
+        banks = [[psum.tile([P, HALF], F32, name=f"bank{h}{n}") for n in range(N_TILES)] for h in range(2)]
+
+        tab_s = tile([P, T // 4], I32, "tab_s")
+        tab_w = [tile([P, T], I32, f"tab_w{a}") for a in range(PASSES)]
+        pick_s = {}
+        pick_w = {}
+        wx_s = tile([P, N // 4], I32, "wx_s")
+        wx_w = tile([P, PASSES, N], I32, "wx_w")
+        bias = tile([P, N_TILES], F32, "bias")
+        wt_raw = [[tile([P, PACK, N // 2], F32, f"wt_raw{a}{u}") for u in range(2)] for a in range(PASSES)]
+        wt_bf = {}
+        wq_w = [[None, None], [None, None]]
+        wq_s = [[tile([P, N // 2], U8, f"wq_s{a}{u}") for u in range(2)] for a in range(PASSES)]
+        wr_bf = [[tile([P, N // 2, PACK], BF16, f"wr_bf{a}{u}") for u in range(2)] for a in range(PASSES)]
+        wr_w = [[tile([P, N // 2], U32, f"wr_w{a}{u}") for u in range(2)] for a in range(PASSES)]
+        wr_s = [[tile([P, N // 2], U8, f"wr_s{a}{u}") for u in range(2)] for a in range(PASSES)]
+        x_raw = [[tile([P, PACK, HALF], F32, f"x_raw{a}{h}") for h in range(2)] for a in range(PASSES)]
+        xq_w = {}
+        xq_s = [[tile([P, HALF], U8, f"xq_s{a}{h}") for h in range(2)] for a in range(PASSES)]
+        result = [[tile([P, HALF], F32, f"result{h}{n}") for n in range(N_TILES)] for h in range(2)]
+        eye = tile([P, P], BF16, "eye")
+        eye_bf = [tile([P, 2, P, PACK], BF16, f"eye_bf{v}") for v in range(2)]
+        eye_w = tile([P, PACK * P], U32, "eye_w")
+        eye_s = tile([P, PACK * P], U8, "eye_s")
+
+        def load_scales(dst, src):
+            for q in range(4):
+                nc.sync.dma_start(out=dst[32 * q : 32 * q + 8, :], in_=src[:, 4 * q : 4 * q + 4, :].bitcast(I32))
+
+        def load_rows(dst, src, a, cols, planes=slice(0, PACK)):
+            rows = src[a * K_PASS : (a + 1) * K_PASS, cols]
+            nc.sync.dma_start(out=dst, in_=rows.rearrange("(p i) c -> p i c", i=PACK)[:, planes, :])
+
+        def load_wt(a, u, planes=slice(0, PACK)):
+            load_rows(wt_raw[a][u][:, planes, :], wt, a, slice(u * N // 2, (u + 1) * N // 2), planes)
+
+        def load_x(a, h, lo=0, hi=HALF):
+            load_rows(x_raw[a][h][:, :, lo:hi], x, a, slice(h * HALF + lo, h * HALF + hi))
+
+        def load_tab(a):
+            nc.sync.dma_start(out=tab_w[a][:], in_=tab_words[a].rearrange("p t i -> p (t i)").bitcast(I32))
+
+        def rows_view(ap):
+            return ap.rearrange("p i (c r) -> p c i r", r=RUN)
+
+        def cols_view(ap):
+            return ap.rearrange("p (c r) i -> p c i r", r=RUN)
+
+        def cast(engine, dst, src):
+            o, i = cols_view(dst), rows_view(src)
+            if engine == "scalar":
+                nc.scalar.activation(out=o, in_=i, func=IDENTITY)
+            else:
+                nc.vector.tensor_copy(out=o, in_=i)
+
+        def quantize(words, scales, src):
+            nc.vector.quantize_mx(out=words.bitcast(FP8X4), scales=scales, in_=src.rearrange("p c i -> p (c i)"))
+
+        def cast_x(engine, a, h, lo, hi, slot):
+            piece = tile([P, hi - lo, PACK], BF16, f"x_bf{a}{h}{lo}", slot)
+            cast(engine, piece[:], x_raw[a][h][:, :, lo:hi])
+            return (a, h, lo, hi, piece)
+
+        def quantize_x(a, h, lo, hi, piece):
+            quantize(xq_w[a, h][:, lo:hi], xq_s[a][h][:, lo:hi], piece[:])
+
+        def decode(a, n):
+            u, c = divmod(n, 2)
+            cols = slice(c * P, (c + 1) * P)
+            for i in range(PACK):
+                slot = slice(i * P, (i + 1) * P)
+                nc.tensor.matmul_mx(
+                    out=banks[1][2 + c][:, slot],
+                    lhsT=eye_w[:, slot].bitcast(FP8X4),
+                    lhsT_scale=eye_s[:, slot],
+                    rhs=wq_w[a][u][:, cols].bitcast(FP8X4),
+                    rhs_scale=wq_s[a][u][:, cols],
+                    start=True,
+                    stop=True,
+                )
+
+        def residual(a, n):
+            u, c = divmod(n, 2)
+            cols = slice(c * P, (c + 1) * P)
+            nc.vector.tensor_tensor(
+                out=cols_view(wr_bf[a][u][:, cols, :]),
+                in0=rows_view(wt_raw[a][u][:, :, cols]),
+                in1=rows_view(banks[1][2 + c][:].rearrange("p (i c) -> p i c", i=PACK)),
+                op=SUBTRACT,
+            )
+
+        def gather_scales(h, slot):
+            pick_s[h] = tile([P, HALF], U8, f"pick_s{h}", slot)
+            nc.vector.tensor_copy(
+                out=pick_s[h][:],
+                in_=tab_s[:].bitcast(U8).indirect(offsets[:, h * HALF // 16 : (h + 1) * HALF // 16]),
+            )
+
+        def gather_words(a, h, slot):
+            pick_w[a, h] = tile([P, HALF], U32, f"pick_w{a}{h}", slot)
+            nc.vector.tensor_copy(
+                out=pick_w[a, h][:],
+                in_=tab_w[a][:].bitcast(U32).indirect(offsets[:, h * HALF // 16 : (h + 1) * HALF // 16]),
+            )
+
+        def tab_pass(words, scales, a, h, n, start):
+            u, c = divmod(n, 2)
+            cols = slice(c * P, (c + 1) * P)
+            nc.tensor.matmul_mx(
+                out=banks[h][n][:],
+                lhsT=words[a][u][:, cols].bitcast(FP8X4),
+                lhsT_scale=scales[a][u][:, cols],
+                rhs=pick_w[a, h][:].bitcast(FP8X4),
+                rhs_scale=pick_s[h][4 * a :, :],
+                start=start,
+                stop=False,
+            )
+
+        def q_passes(a, h, tiles=range(N_TILES)):
+            for n in tiles:
+                tab_pass(wq_w, wq_s, a, h, n, a == 0)
+
+        def r_passes(a, h, tiles=range(N_TILES)):
+            for n in tiles:
+                tab_pass(wr_w, wr_s, a, h, n, False)
+
+        def x_passes(a, h):
+            for n in range(N_TILES):
+                x_pass(a, h, n)
+
+        def load_wx(a):
+            nc.sync.dma_start(out=wx_w[:, a, :], in_=wx_words[a].rearrange("p n i -> p (n i)").bitcast(I32))
+
+        def x_pass(a, h, n):
+            cols = slice(n * P, (n + 1) * P)
+            nc.tensor.matmul_mx(
+                out=banks[h][n][:],
+                lhsT=wx_w[:, a, cols].bitcast(FP8X4),
+                lhsT_scale=wx_s[4 * a :, :].bitcast(U8)[:, cols],
+                rhs=xq_w[a, h][:].bitcast(FP8X4),
+                rhs_scale=xq_s[a][h][:],
+                start=False,
+                stop=(a == PASSES - 1),
+            )
+
+        def finish(engine, h, n):
+            if engine == "scalar":
+                nc.scalar.activation(out=result[h][n][:], in_=banks[h][n][:], func=IDENTITY, bias=bias[:, n : n + 1])
+            else:
+                nc.vector.tensor_scalar(
+                    out=result[h][n][:], in0=banks[h][n][:], scalar1=bias[:, n : n + 1], scalar2=None, op0=ADD
+                )
+            nc.sync.dma_start(out=out[n * P : (n + 1) * P, h * HALF : (h + 1) * HALF], in_=result[h][n][:])
+
+        nc.vector.memset(tab_s[:], 0)
+        nc.sync.dma_start(offsets[:], offs)
+        load_scales(tab_s, tab_scales)
+        load_wt(0, 0)
+        load_wt(0, 1)
+        with nc.allow_non_contiguous_dma(reason="one bias value for each partition and output tile"):
+            nc.sync.dma_start(out=bias[:], in_=b.rearrange("(n p) -> p n", p=P))
+        load_tab(0)
+        load_wt(1, 0)
+        load_wt(1, 1)
+        load_x(0, 0)
+        load_tab(1)
+        for v in range(2):
+            nc.vector.memset(eye_bf[v][:].rearrange("p i m t -> p (i m t)").bitcast(I32), 0)
+        nc.vector.memset(wx_s[:], 0)
+        load_scales(wx_s, wx_scales)
+        load_wx(0)
+        load_x(1, 0)
+        load_wx(1)
+        load_x(0, 1)
+        load_x(1, 1, 0, QUARTER)
+        load_x(1, 1, QUARTER, HALF)
+
+        make_identity(nc, eye[:])
+        for i in range(PACK):
+            nc.scalar.activation(out=eye_bf[i // 2][:, i % 2, :, i], in_=eye[:], func=IDENTITY)
+        for v in range(2):
+            cols = slice(2 * v * P, 2 * (v + 1) * P)
+            quantize(eye_w[:, cols], eye_s[:, cols], eye_bf[v][:].rearrange("p i m t -> p (i m) t"))
+
+        def first_tier(a, u, slot_bf, slot_w):
+            wt_bf[a, u] = tile([P, N // 2, PACK], BF16, f"wt_bf{a}{u}", slot_bf)
+            wq_w[a][u] = tile([P, N // 2], U32, f"wq_w{a}{u}", slot_w)
+            cast("scalar", wt_bf[a, u][:], wt_raw[a][u][:])
+            quantize(wq_w[a][u][:], wq_s[a][u][:], wt_bf[a, u][:])
+
+        def leftover(a, u):
+            for n in (2 * u, 2 * u + 1):
+                decode(a, n)
+                residual(a, n)
+
+        def second_tier(a, u):
+            quantize(wr_w[a][u][:], wr_s[a][u][:], wr_bf[a][u][:])
+
+        first_tier(0, 0, "eye", None)
+        first_tier(0, 1, "eye_bf0", "eye_bf1")
+        gather_scales(0, None)
+        gather_scales(1, None)
+        leftover(0, 0)
+        gather_words(0, 0, "wt_raw00")
+        leftover(0, 1)
+        second_tier(0, 0)
+        second_tier(0, 1)
+        first_tier(1, 0, "eye", "wt_raw01")
+        first_tier(1, 1, "eye_bf0", "wr_bf00")
+        gather_words(0, 1, "wr_bf01")
+        leftover(1, 0)
+        second_tier(1, 0)
+        x00 = cast_x("scalar", 0, 0, 0, HALF, "eye")
+        xq_w[0, 0] = tile([P, HALF], U32, "xq_w00", "wt_raw10")
+        quantize_x(*x00)
+        gather_words(1, 0, "wr_bf10")
+        leftover(1, 1)
+        second_tier(1, 1)
+        gather_words(1, 1, "wr_bf11")
+
+        q_passes(0, 0)
+        r_passes(0, 0)
+        q_passes(0, 1, (0, 1))
+        r_passes(0, 1, (0, 1))
+        x_passes(0, 0)
+        q_passes(1, 0)
+        r_passes(1, 0)
+
+        x10 = cast_x("scalar", 1, 0, 0, HALF, "x_raw00")
+        xq_w[1, 0] = tile([P, HALF], U32, "xq_w10", "tab_w1")
+        quantize_x(*x10)
+        x_passes(1, 0)
+        q_passes(0, 1, (2, 3))
+        r_passes(0, 1, (2, 3))
+        q_passes(1, 1)
+        r_passes(1, 1)
+
+        xq_w[0, 1] = tile([P, HALF], U32, "xq_w01")
+        xq_w[1, 1] = tile([P, HALF], U32, "xq_w11")
+        x01a = cast_x("scalar", 0, 1, 0, QUARTER, "x_raw10")
+        x01b = cast_x("vector", 0, 1, QUARTER, HALF, "x_raw00")
+        for n in range(N_TILES):
+            finish("scalar", 0, n)
+        quantize_x(*x01b)
+        quantize_x(*x01a)
+        x_passes(0, 1)
+        x11a = cast_x("vector", 1, 1, 0, QUARTER, "x_raw00")
+        x11b = cast_x("vector", 1, 1, QUARTER, HALF, "x_raw10")
+        quantize_x(*x11a)
+        quantize_x(*x11b)
+        for n in range(N_TILES):
+            x_pass(1, 1, n)
+            finish("scalar" if n % 2 == 0 else "vector", 1, n)

@@ -1,7 +1,6 @@
 from contextlib import ExitStack
 
 import concourse.mybir as mybir
-from concourse.masks import make_identity
 
 K, L, N, T, J = 1024, 1024, 512, 2048, 1024
 FLOPS = 3758096384
@@ -48,19 +47,21 @@ def tile_list_tiert_bias_kernel(
         wx_s = tile([P, N // 4], I32, "wx_s")
         wx_w = tile([P, PASSES, N], I32, "wx_w")
         bias = tile([P, N_TILES], F32, "bias")
-        wt_raw = [[tile([P, PACK, N // 2], F32, f"wt_raw{a}{u}") for u in range(2)] for a in range(PASSES)]
+        wt_first = [tile([P, PACK, N // 2], F32, f"wt_raw0{u}") for u in range(2)]
+        wt_second = tile([P, PACK, N], F32, "wt_raw1")
+        wt_raw = [[t[:] for t in wt_first], [wt_second[:, :, u * N // 2 : (u + 1) * N // 2] for u in range(2)]]
         wt_bf = {}
         wq_w = [[None, None], [None, None]]
         wq_s = [[tile([P, N // 2], U8, f"wq_s{a}{u}") for u in range(2)] for a in range(PASSES)]
-        wr_bf = [[tile([P, N // 2, PACK], BF16, f"wr_bf{a}{u}") for u in range(2)] for a in range(PASSES)]
+        wr_bf = [[None, None], [None, None]]
         wr_w = [[tile([P, N // 2], U32, f"wr_w{a}{u}") for u in range(2)] for a in range(PASSES)]
         wr_s = [[tile([P, N // 2], U8, f"wr_s{a}{u}") for u in range(2)] for a in range(PASSES)]
         x_raw = [[tile([P, PACK, HALF], F32, f"x_raw{a}{h}") for h in range(2)] for a in range(PASSES)]
         xq_w = {}
         xq_s = [[tile([P, HALF], U8, f"xq_s{a}{h}") for h in range(2)] for a in range(PASSES)]
         result = [[tile([P, HALF], F32, f"result{h}{n}") for n in range(N_TILES)] for h in range(2)]
-        eye = tile([P, P], BF16, "eye")
-        eye_bf = [tile([P, 2, P, PACK], BF16, f"eye_bf{v}") for v in range(2)]
+        eye = tile([P, K_PASS + PACK], BF16, "eye")
+        eye_bf = [tile([P, 2, K_PASS], BF16, f"eye_bf{v}") for v in range(2)]
         eye_w = tile([P, PACK * P], U32, "eye_w")
         eye_s = tile([P, PACK * P], U8, "eye_s")
 
@@ -72,8 +73,6 @@ def tile_list_tiert_bias_kernel(
             rows = src[a * K_PASS : (a + 1) * K_PASS, cols]
             nc.sync.dma_start(out=dst, in_=rows.rearrange("(p i) c -> p i c", i=PACK)[:, planes, :])
 
-        def load_wt(a, u, planes=slice(0, PACK)):
-            load_rows(wt_raw[a][u][:, planes, :], wt, a, slice(u * N // 2, (u + 1) * N // 2), planes)
 
         def load_x(a, h, lo=0, hi=HALF):
             load_rows(x_raw[a][h][:, :, lo:hi], x, a, slice(h * HALF + lo, h * HALF + hi))
@@ -100,10 +99,10 @@ def tile_list_tiert_bias_kernel(
         def cast_x(engine, a, h, lo, hi, slot):
             piece = tile([P, hi - lo, PACK], BF16, f"x_bf{a}{h}{lo}", slot)
             cast(engine, piece[:], x_raw[a][h][:, :, lo:hi])
-            return (a, h, lo, hi, piece)
+            return (a, h, lo, hi, piece[:])
 
         def quantize_x(a, h, lo, hi, piece):
-            quantize(xq_w[a, h][:, lo:hi], xq_s[a][h][:, lo:hi], piece[:])
+            quantize(xq_w[a, h][:, lo:hi], xq_s[a][h][:, lo:hi], piece)
 
         def decode(a, n):
             u, c = divmod(n, 2)
@@ -111,7 +110,7 @@ def tile_list_tiert_bias_kernel(
             for i in range(PACK):
                 slot = slice(i * P, (i + 1) * P)
                 nc.tensor.matmul_mx(
-                    out=banks[1][2 + c][:, slot],
+                    out=banks[1][n if a == 0 else 2 + c][:, slot],
                     lhsT=eye_w[:, slot].bitcast(FP8X4),
                     lhsT_scale=eye_s[:, slot],
                     rhs=wq_w[a][u][:, cols].bitcast(FP8X4),
@@ -126,7 +125,7 @@ def tile_list_tiert_bias_kernel(
             nc.vector.tensor_tensor(
                 out=cols_view(wr_bf[a][u][:, cols, :]),
                 in0=rows_view(wt_raw[a][u][:, :, cols]),
-                in1=rows_view(banks[1][2 + c][:].rearrange("p (i c) -> p i c", i=PACK)),
+                in1=rows_view(banks[1][n if a == 0 else 2 + c][:].rearrange("p (i c) -> p i c", i=PACK)),
                 op=SUBTRACT,
             )
 
@@ -144,7 +143,7 @@ def tile_list_tiert_bias_kernel(
                 in_=tab_w[a][:].bitcast(U32).indirect(offsets[:, h * HALF // 16 : (h + 1) * HALF // 16]),
             )
 
-        def tab_pass(words, scales, a, h, n, start):
+        def tab_pass(words, scales, a, h, n, start, stop=False):
             u, c = divmod(n, 2)
             cols = slice(c * P, (c + 1) * P)
             nc.tensor.matmul_mx(
@@ -154,7 +153,7 @@ def tile_list_tiert_bias_kernel(
                 rhs=pick_w[a, h][:].bitcast(FP8X4),
                 rhs_scale=pick_s[h][4 * a :, :],
                 start=start,
-                stop=False,
+                stop=stop,
             )
 
         def q_passes(a, h, tiles=range(N_TILES)):
@@ -165,23 +164,23 @@ def tile_list_tiert_bias_kernel(
             for n in tiles:
                 tab_pass(wr_w, wr_s, a, h, n, False)
 
-        def x_passes(a, h):
-            for n in range(N_TILES):
+        def x_passes(a, h, tiles=range(N_TILES)):
+            for n in tiles:
                 x_pass(a, h, n)
 
         def load_wx(a):
             nc.sync.dma_start(out=wx_w[:, a, :], in_=wx_words[a].rearrange("p n i -> p (n i)").bitcast(I32))
 
-        def x_pass(a, h, n):
+        def x_pass(a, h, n, start=False, stop=False, part=slice(0, HALF)):
             cols = slice(n * P, (n + 1) * P)
             nc.tensor.matmul_mx(
-                out=banks[h][n][:],
+                out=banks[h][n][:, part],
                 lhsT=wx_w[:, a, cols].bitcast(FP8X4),
                 lhsT_scale=wx_s[4 * a :, :].bitcast(U8)[:, cols],
-                rhs=xq_w[a, h][:].bitcast(FP8X4),
-                rhs_scale=xq_s[a][h][:],
-                start=False,
-                stop=(a == PASSES - 1),
+                rhs=xq_w[a, h][:, part].bitcast(FP8X4),
+                rhs_scale=xq_s[a][h][:, part],
+                start=start,
+                stop=stop,
             )
 
         def finish(engine, h, n):
@@ -196,40 +195,47 @@ def tile_list_tiert_bias_kernel(
         nc.vector.memset(tab_s[:], 0)
         nc.sync.dma_start(offsets[:], offs)
         load_scales(tab_s, tab_scales)
-        load_wt(0, 0)
-        load_wt(0, 1)
+        for u in range(2):
+            load_rows(wt_raw[0][u], wt, 0, slice(u * N // 2, (u + 1) * N // 2))
+        load_tab(0)
+        load_rows(wt_second[:], wt, 1, slice(0, N))
         with nc.allow_non_contiguous_dma(reason="one bias value for each partition and output tile"):
             nc.sync.dma_start(out=bias[:], in_=b.rearrange("(n p) -> p n", p=P))
-        load_tab(0)
-        load_wt(1, 0)
-        load_wt(1, 1)
         load_x(0, 0)
-        load_tab(1)
-        for v in range(2):
-            nc.vector.memset(eye_bf[v][:].rearrange("p i m t -> p (i m t)").bitcast(I32), 0)
         nc.vector.memset(wx_s[:], 0)
         load_scales(wx_s, wx_scales)
         load_wx(0)
+        load_tab(1)
         load_x(1, 0)
         load_wx(1)
         load_x(0, 1)
         load_x(1, 1, 0, QUARTER)
         load_x(1, 1, QUARTER, HALF)
 
-        make_identity(nc, eye[:])
+        nc.gpsimd.memset(eye[:], 0.0)
+        nc.gpsimd.affine_select(
+            out=eye[:],
+            in_=eye[:],
+            compare_op=mybir.AluOpType.not_equal,
+            fill=1.0,
+            base=PACK - 1,
+            pattern=[[-1, K_PASS + PACK]],
+            channel_multiplier=PACK,
+        )
         for i in range(PACK):
-            nc.scalar.activation(out=eye_bf[i // 2][:, i % 2, :, i], in_=eye[:], func=IDENTITY)
+            nc.vector.tensor_copy(out=eye_bf[i // 2][:, i % 2, :], in_=eye[:, PACK - 1 - i : PACK - 1 - i + K_PASS])
         for v in range(2):
             cols = slice(2 * v * P, 2 * (v + 1) * P)
-            quantize(eye_w[:, cols], eye_s[:, cols], eye_bf[v][:].rearrange("p i m t -> p (i m) t"))
+            quantize(eye_w[:, cols], eye_s[:, cols], eye_bf[v][:])
 
         def first_tier(a, u, slot_bf, slot_w):
             wt_bf[a, u] = tile([P, N // 2, PACK], BF16, f"wt_bf{a}{u}", slot_bf)
             wq_w[a][u] = tile([P, N // 2], U32, f"wq_w{a}{u}", slot_w)
-            cast("scalar", wt_bf[a, u][:], wt_raw[a][u][:])
+            cast("scalar", wt_bf[a, u][:], wt_raw[a][u])
             quantize(wq_w[a][u][:], wq_s[a][u][:], wt_bf[a, u][:])
 
-        def leftover(a, u):
+        def leftover(a, u, slot=None):
+            wr_bf[a][u] = tile([P, N // 2, PACK], BF16, f"wr_bf{a}{u}", slot)
             for n in (2 * u, 2 * u + 1):
                 decode(a, n)
                 residual(a, n)
@@ -237,27 +243,30 @@ def tile_list_tiert_bias_kernel(
         def second_tier(a, u):
             quantize(wr_w[a][u][:], wr_s[a][u][:], wr_bf[a][u][:])
 
-        first_tier(0, 0, "eye", None)
-        first_tier(0, 1, "eye_bf0", "eye_bf1")
-        gather_scales(0, None)
-        gather_scales(1, None)
+        gather_scales(0, "eye_bf0")
+        first_tier(0, 0, None, "eye_bf1")
+        first_tier(0, 1, None, "wt_bf00")
+        gather_scales(1, "eye")
         leftover(0, 0)
         gather_words(0, 0, "wt_raw00")
         leftover(0, 1)
         second_tier(0, 0)
         second_tier(0, 1)
-        first_tier(1, 0, "eye", "wt_raw01")
-        first_tier(1, 1, "eye_bf0", "wr_bf00")
+        first_tier(1, 0, None, "wt_raw01")
+        first_tier(1, 1, None, "wr_bf00")
         gather_words(0, 1, "wr_bf01")
         leftover(1, 0)
-        second_tier(1, 0)
-        x00 = cast_x("scalar", 0, 0, 0, HALF, "eye")
-        xq_w[0, 0] = tile([P, HALF], U32, "xq_w00", "wt_raw10")
+        x00 = cast_x("scalar", 0, 0, 0, HALF, None)
+        xq_w[0, 0] = tile([P, HALF], U32, "xq_w00", "wt_bf11")
         quantize_x(*x00)
+        second_tier(1, 0)
         gather_words(1, 0, "wr_bf10")
         leftover(1, 1)
+        gather_words(1, 1, "wt_raw1")
         second_tier(1, 1)
-        gather_words(1, 1, "wr_bf11")
+        x10 = cast_x("scalar", 1, 0, 0, HALF, "x_raw00")
+        xq_w[1, 0] = tile([P, HALF], U32, "xq_w10", "tab_w1")
+        quantize_x(*x10)
 
         q_passes(0, 0)
         r_passes(0, 0)
@@ -266,29 +275,27 @@ def tile_list_tiert_bias_kernel(
         x_passes(0, 0)
         q_passes(1, 0)
         r_passes(1, 0)
-
-        x10 = cast_x("scalar", 1, 0, 0, HALF, "x_raw00")
-        xq_w[1, 0] = tile([P, HALF], U32, "xq_w10", "tab_w1")
-        quantize_x(*x10)
-        x_passes(1, 0)
+        for n in range(N_TILES):
+            x_pass(1, 0, n, stop=True)
         q_passes(0, 1, (2, 3))
         r_passes(0, 1, (2, 3))
         q_passes(1, 1)
         r_passes(1, 1)
 
-        xq_w[0, 1] = tile([P, HALF], U32, "xq_w01")
-        xq_w[1, 1] = tile([P, HALF], U32, "xq_w11")
-        x01a = cast_x("scalar", 0, 1, 0, QUARTER, "x_raw10")
-        x01b = cast_x("vector", 0, 1, QUARTER, HALF, "x_raw00")
+        x01 = cast_x("scalar", 0, 1, 0, HALF, "x_raw10")
         for n in range(N_TILES):
             finish("scalar", 0, n)
-        quantize_x(*x01b)
-        quantize_x(*x01a)
-        x_passes(0, 1)
-        x11a = cast_x("vector", 1, 1, 0, QUARTER, "x_raw00")
-        x11b = cast_x("vector", 1, 1, QUARTER, HALF, "x_raw10")
-        quantize_x(*x11a)
-        quantize_x(*x11b)
+        x11 = tile([P, HALF, PACK], BF16, "x_bf11", "wr_bf11")
+        for lo in (0, QUARTER):
+            cast("vector", x11[:, lo : lo + QUARTER, :], x_raw[1][1][:, :, lo : lo + QUARTER])
+        xq_w[0, 1] = tile([P, HALF], U32, "xq_w01", "x_raw00")
+        xq_w[1, 1] = tile([P, HALF], U32, "xq_w11")
+        quantize_x(1, 1, 0, QUARTER, x11[:, :QUARTER, :])
+        quantize_x(*x01)
+        quantize_x(1, 1, QUARTER, HALF, x11[:, QUARTER:, :])
         for n in range(N_TILES):
-            x_pass(1, 1, n)
+            x_pass(1, 1, n, part=slice(0, QUARTER))
+        x_passes(0, 1)
+        for n in range(N_TILES):
+            x_pass(1, 1, n, stop=True, part=slice(QUARTER, HALF))
             finish("scalar" if n % 2 == 0 else "vector", 1, n)

@@ -54,12 +54,12 @@ def tile_list_tiert_bias_kernel(
         wq_w = [[None, None], [None, None]]
         wq_s = [[tile([P, N // 2], U8, f"wq_s{a}{u}") for u in range(2)] for a in range(PASSES)]
         wr_bf = [[None, None], [None, None]]
-        wr_w = [[tile([P, N // 2], U32, f"wr_w{a}{u}") for u in range(2)] for a in range(PASSES)]
+        wr_w = [[None, None], [None, None]]
         wr_s = [[tile([P, N // 2], U8, f"wr_s{a}{u}") for u in range(2)] for a in range(PASSES)]
         x_raw = [[tile([P, PACK, HALF], F32, f"x_raw{a}{h}") for h in range(2)] for a in range(PASSES)]
         xq_w = {}
         xq_s = [[tile([P, HALF], U8, f"xq_s{a}{h}") for h in range(2)] for a in range(PASSES)]
-        result = [[tile([P, HALF], F32, f"result{h}{n}") for n in range(N_TILES)] for h in range(2)]
+        result = [None, None]
         eye = tile([P, K_PASS + PACK], BF16, "eye")
         eye_bf = [tile([P, 2, K_PASS], BF16, f"eye_bf{v}") for v in range(2)]
         eye_w = tile([P, PACK * P], U32, "eye_w")
@@ -160,9 +160,9 @@ def tile_list_tiert_bias_kernel(
             for n in tiles:
                 tab_pass(wq_w, wq_s, a, h, n, a == 0)
 
-        def r_passes(a, h, tiles=range(N_TILES)):
+        def r_passes(a, h, tiles=range(N_TILES), stop=False):
             for n in tiles:
-                tab_pass(wr_w, wr_s, a, h, n, False)
+                tab_pass(wr_w, wr_s, a, h, n, False, stop)
 
         def x_passes(a, h, tiles=range(N_TILES)):
             for n in tiles:
@@ -185,12 +185,12 @@ def tile_list_tiert_bias_kernel(
 
         def finish(engine, h, n):
             if engine == "scalar":
-                nc.scalar.activation(out=result[h][n][:], in_=banks[h][n][:], func=IDENTITY, bias=bias[:, n : n + 1])
+                nc.scalar.activation(out=result[h][:, n, :], in_=banks[h][n][:], func=IDENTITY, bias=bias[:, n : n + 1])
             else:
                 nc.vector.tensor_scalar(
-                    out=result[h][n][:], in0=banks[h][n][:], scalar1=bias[:, n : n + 1], scalar2=None, op0=ADD
+                    out=result[h][:, n, :], in0=banks[h][n][:], scalar1=bias[:, n : n + 1], scalar2=None, op0=ADD
                 )
-            nc.sync.dma_start(out=out[n * P : (n + 1) * P, h * HALF : (h + 1) * HALF], in_=result[h][n][:])
+            nc.sync.dma_start(out=out[n * P : (n + 1) * P, h * HALF : (h + 1) * HALF], in_=result[h][:, n, :])
 
         nc.vector.memset(tab_s[:], 0)
         nc.sync.dma_start(offsets[:], offs)
@@ -201,13 +201,13 @@ def tile_list_tiert_bias_kernel(
         load_rows(wt_second[:], wt, 1, slice(0, N))
         with nc.allow_non_contiguous_dma(reason="one bias value for each partition and output tile"):
             nc.sync.dma_start(out=bias[:], in_=b.rearrange("(n p) -> p n", p=P))
-        load_x(0, 0)
         nc.vector.memset(wx_s[:], 0)
         load_scales(wx_s, wx_scales)
         load_wx(0)
+        load_x(0, 0)
         load_tab(1)
-        load_x(1, 0)
         load_wx(1)
+        load_x(1, 0)
         load_x(0, 1)
         load_x(1, 1, 0, QUARTER)
         load_x(1, 1, QUARTER, HALF)
@@ -240,62 +240,66 @@ def tile_list_tiert_bias_kernel(
                 decode(a, n)
                 residual(a, n)
 
-        def second_tier(a, u):
+        def second_tier(a, u, slot=None):
+            wr_w[a][u] = tile([P, N // 2], U32, f"wr_w{a}{u}", slot)
             quantize(wr_w[a][u][:], wr_s[a][u][:], wr_bf[a][u][:])
 
         gather_scales(0, "eye_bf0")
         first_tier(0, 0, None, "eye_bf1")
-        first_tier(0, 1, None, "wt_bf00")
-        gather_scales(1, "eye")
+        gather_scales(1, "wt_bf00")
+        first_tier(0, 1, None, "tab_s")
         leftover(0, 0)
-        gather_words(0, 0, "wt_raw00")
+        gather_words(0, 0, "wt_bf01")
         leftover(0, 1)
+        q_passes(0, 0)
+        first_tier(1, 0, None, "wt_raw00")
         second_tier(0, 0)
         second_tier(0, 1)
-        first_tier(1, 0, None, "wt_raw01")
         first_tier(1, 1, None, "wr_bf00")
         gather_words(0, 1, "wr_bf01")
-        leftover(1, 0)
-        x00 = cast_x("scalar", 0, 0, 0, HALF, None)
-        xq_w[0, 0] = tile([P, HALF], U32, "xq_w00", "wt_bf11")
-        quantize_x(*x00)
-        second_tier(1, 0)
-        gather_words(1, 0, "wr_bf10")
-        leftover(1, 1)
-        gather_words(1, 1, "wt_raw1")
-        second_tier(1, 1)
-        x10 = cast_x("scalar", 1, 0, 0, HALF, "x_raw00")
-        xq_w[1, 0] = tile([P, HALF], U32, "xq_w10", "tab_w1")
-        quantize_x(*x10)
-
-        q_passes(0, 0)
         r_passes(0, 0)
+        leftover(1, 0)
         q_passes(0, 1, (0, 1))
         r_passes(0, 1, (0, 1))
+        x00 = cast_x("scalar", 0, 0, 0, HALF, None)
+        xq_w[0, 0] = tile([P, HALF], U32, "xq_w00", "tab_w0")
+        quantize_x(*x00)
+        gather_words(1, 0, "x_raw00")
+        leftover(1, 1, "x_bf000")
         x_passes(0, 0)
         q_passes(1, 0)
-        r_passes(1, 0)
-        for n in range(N_TILES):
-            x_pass(1, 0, n, stop=True)
         q_passes(0, 1, (2, 3))
         r_passes(0, 1, (2, 3))
-        q_passes(1, 1)
-        r_passes(1, 1)
+        second_tier(1, 0, "wt_raw1")
+        second_tier(1, 1)
+        gather_words(1, 1, "wr_bf10")
+        r_passes(1, 0)
+        xq_w[1, 0] = tile([P, HALF], U32, "xq_w10", "tab_w1")
+        quantize_x(*cast_x("scalar", 1, 0, 0, HALF, None))
+        for n in range(N_TILES):
+            x_pass(1, 0, n, stop=True)
 
-        x01 = cast_x("scalar", 0, 1, 0, HALF, "x_raw10")
+        x01 = cast_x("scalar", 0, 1, 0, HALF, None)
+        result[0] = tile([P, N_TILES, HALF], F32, "result0", "x_raw01")
+        result[1] = tile([P, N_TILES, HALF], F32, "result1")
         for n in range(N_TILES):
             finish("scalar", 0, n)
-        x11 = tile([P, HALF, PACK], BF16, "x_bf11", "wr_bf11")
-        for lo in (0, QUARTER):
-            cast("vector", x11[:, lo : lo + QUARTER, :], x_raw[1][1][:, :, lo : lo + QUARTER])
-        xq_w[0, 1] = tile([P, HALF], U32, "xq_w01", "x_raw00")
+        xq_w[0, 1] = tile([P, HALF], U32, "xq_w01")
         xq_w[1, 1] = tile([P, HALF], U32, "xq_w11")
-        quantize_x(1, 1, 0, QUARTER, x11[:, :QUARTER, :])
+        x11a = cast_x("vector", 1, 1, 0, QUARTER, "x_bf100")
         quantize_x(*x01)
-        quantize_x(1, 1, QUARTER, HALF, x11[:, QUARTER:, :])
-        for n in range(N_TILES):
-            x_pass(1, 1, n, part=slice(0, QUARTER))
+        quantize_x(*x11a)
+        x11b = cast_x("vector", 1, 1, QUARTER, HALF, "x_bf010")
+        quantize_x(*x11b)
+        q_passes(1, 1, (0, 1, 2))
+        r_passes(1, 1, (0,))
         x_passes(0, 1)
         for n in range(N_TILES):
-            x_pass(1, 1, n, stop=True, part=slice(QUARTER, HALF))
-            finish("scalar" if n % 2 == 0 else "vector", 1, n)
+            x_pass(1, 1, n, part=slice(0, QUARTER))
+        for n in range(N_TILES):
+            x_pass(1, 1, n, stop=n == 0, part=slice(QUARTER, HALF))
+            if n == 3:
+                q_passes(1, 1, (n,))
+            if n > 0:
+                r_passes(1, 1, (n,), stop=True)
+            finish("scalar" if n % 2 == 1 else "vector", 1, n)

@@ -21,9 +21,10 @@ PACK = 4
 K_PASS = P * PACK
 PASSES = K // K_PASS
 N_TILES = N // P
-HALF = J // 2
-QUARTER = J // 4
+BANK = 512
 RUN = 4
+GROUPS = (slice(0, 512), slice(512, 768), slice(768, 1024))
+FIRST, MIDDLE, LAST = range(3)
 
 
 def tile_list_tiert_bias_kernel(
@@ -37,29 +38,46 @@ def tile_list_tiert_bias_kernel(
         def tile(shape, dtype, name, slot=None):
             return sb.tile(shape, dtype, name=name, tag=slot or name, align_bytes=64)
 
+        def width(g):
+            return GROUPS[g].stop - GROUPS[g].start
+
         offsets = sb.tile([P, J // 16], U16, name="offsets")
-        banks = [[psum.tile([P, HALF], F32, name=f"bank{h}{n}") for n in range(N_TILES)] for h in range(2)]
+        banks = [psum.tile([P, BANK], F32, name=f"bank{i}") for i in range(8)]
+
+        def sums(g, n):
+            first = GROUPS[g].start * N_TILES + n * width(g)
+            bank, col = divmod(first, BANK)
+            return banks[bank][:, col : col + width(g)]
+
+        def opens_bank(g, n):
+            return n * width(g) % BANK == 0
+
+        def closes_bank(g, n):
+            return (n + 1) * width(g) % BANK == 0
+
+        def scratch_bank(a, n):
+            return banks[4 + n if a == 0 else 6 + n % 2]
 
         tab_s = tile([P, T // 4], I32, "tab_s")
         tab_w = [tile([P, T], I32, f"tab_w{a}") for a in range(PASSES)]
         pick_s = {}
         pick_w = {}
         wx_s = tile([P, N // 4], I32, "wx_s")
-        wx_w = tile([P, PASSES, N], I32, "wx_w")
+        wx_w = [tile([P, N], I32, f"wx_w{a}") for a in range(PASSES)]
         bias = tile([P, N_TILES], F32, "bias")
         wt_first = [tile([P, PACK, N // 2], F32, f"wt_raw0{u}") for u in range(2)]
         wt_second = tile([P, PACK, N], F32, "wt_raw1")
         wt_raw = [[t[:] for t in wt_first], [wt_second[:, :, u * N // 2 : (u + 1) * N // 2] for u in range(2)]]
-        wt_bf = {}
-        wq_w = [[None, None], [None, None]]
-        wq_s = [[tile([P, N // 2], U8, f"wq_s{a}{u}") for u in range(2)] for a in range(PASSES)]
-        wr_bf = [[None, None], [None, None]]
-        wr_w = [[None, None], [None, None]]
-        wr_s = [[tile([P, N // 2], U8, f"wr_s{a}{u}") for u in range(2)] for a in range(PASSES)]
-        x_raw = [[tile([P, PACK, HALF], F32, f"x_raw{a}{h}") for h in range(2)] for a in range(PASSES)]
+        wq_w = {}
+        wq_s = {(a, u): tile([P, N // 2], U8, f"wq_s{a}{u}") for a in range(PASSES) for u in range(2)}
+        wr_bf = {}
+        wr_w = {}
+        wr_s = {(a, u): tile([P, N // 2], U8, f"wr_s{a}{u}") for a in range(PASSES) for u in range(2)}
+        x_raw = {(a, g): tile([P, PACK, width(g)], F32, f"x_raw{a}{g}") for a in range(PASSES) for g in range(3)}
+        x_bf = {}
         xq_w = {}
-        xq_s = [[tile([P, HALF], U8, f"xq_s{a}{h}") for h in range(2)] for a in range(PASSES)]
-        result = [None, None]
+        xq_s = {(a, g): tile([P, width(g)], U8, f"xq_s{a}{g}") for a in range(PASSES) for g in range(3)}
+        result = {}
         eye = tile([P, K_PASS + PACK], BF16, "eye")
         eye_bf = [tile([P, 2, K_PASS], BF16, f"eye_bf{v}") for v in range(2)]
         eye_w = tile([P, PACK * P], U32, "eye_w")
@@ -69,16 +87,15 @@ def tile_list_tiert_bias_kernel(
             for q in range(4):
                 nc.sync.dma_start(out=dst[32 * q : 32 * q + 8, :], in_=src[:, 4 * q : 4 * q + 4, :].bitcast(I32))
 
-        def load_rows(dst, src, a, cols, planes=slice(0, PACK)):
+        def load_rows(dst, src, a, cols):
             rows = src[a * K_PASS : (a + 1) * K_PASS, cols]
-            nc.sync.dma_start(out=dst, in_=rows.rearrange("(p i) c -> p i c", i=PACK)[:, planes, :])
+            nc.sync.dma_start(out=dst, in_=rows.rearrange("(p i) c -> p i c", i=PACK))
 
+        def load_x(a, g):
+            load_rows(x_raw[a, g][:], x, a, GROUPS[g])
 
-        def load_x(a, h, lo=0, hi=HALF):
-            load_rows(x_raw[a][h][:, :, lo:hi], x, a, slice(h * HALF + lo, h * HALF + hi))
-
-        def load_tab(a):
-            nc.sync.dma_start(out=tab_w[a][:], in_=tab_words[a].rearrange("p t i -> p (t i)").bitcast(I32))
+        def load_words(dst, src):
+            nc.sync.dma_start(out=dst[:], in_=src.rearrange("p t i -> p (t i)").bitcast(I32))
 
         def rows_view(ap):
             return ap.rearrange("p i (c r) -> p c i r", r=RUN)
@@ -87,130 +104,142 @@ def tile_list_tiert_bias_kernel(
             return ap.rearrange("p (c r) i -> p c i r", r=RUN)
 
         def cast(engine, dst, src):
-            o, i = cols_view(dst), rows_view(src)
             if engine == "scalar":
-                nc.scalar.activation(out=o, in_=i, func=IDENTITY)
+                nc.scalar.activation(out=cols_view(dst), in_=rows_view(src), func=IDENTITY)
             else:
-                nc.vector.tensor_copy(out=o, in_=i)
+                nc.vector.tensor_copy(out=cols_view(dst), in_=rows_view(src))
 
         def quantize(words, scales, src):
             nc.vector.quantize_mx(out=words.bitcast(FP8X4), scales=scales, in_=src.rearrange("p c i -> p (c i)"))
 
-        def cast_x(engine, a, h, lo, hi, slot):
-            piece = tile([P, hi - lo, PACK], BF16, f"x_bf{a}{h}{lo}", slot)
-            cast(engine, piece[:], x_raw[a][h][:, :, lo:hi])
-            return (a, h, lo, hi, piece[:])
+        def cast_x(a, g, engines, slot=None):
+            x_bf[a, g] = tile([P, width(g), PACK], BF16, f"x_bf{a}{g}", slot)
+            share = width(g) // len(engines)
+            for s, engine in enumerate(engines):
+                cols = slice(s * share, (s + 1) * share)
+                cast(engine, x_bf[a, g][:, cols, :], x_raw[a, g][:, :, cols])
 
-        def quantize_x(a, h, lo, hi, piece):
-            quantize(xq_w[a, h][:, lo:hi], xq_s[a][h][:, lo:hi], piece)
+        def quantize_x(a, g, slot=None):
+            xq_w[a, g] = tile([P, width(g)], U32, f"xq_w{a}{g}", slot)
+            quantize(xq_w[a, g][:], xq_s[a, g][:], x_bf[a, g][:])
 
-        def decode(a, n):
+        def first_tier(a, u, slot=None):
+            wt_bf = tile([P, N // 2, PACK], BF16, f"wt_bf{a}{u}")
+            wq_w[a, u] = tile([P, N // 2], U32, f"wq_w{a}{u}", slot)
+            cast("scalar", wt_bf[:], wt_raw[a][u])
+            quantize(wq_w[a, u][:], wq_s[a, u][:], wt_bf[:])
+
+        def leftover(a, n, slot=None):
             u, c = divmod(n, 2)
             cols = slice(c * P, (c + 1) * P)
+            if c == 0:
+                wr_bf[a, u] = tile([P, N // 2, PACK], BF16, f"wr_bf{a}{u}", slot)
             for i in range(PACK):
-                slot = slice(i * P, (i + 1) * P)
+                part = slice(i * P, (i + 1) * P)
                 nc.tensor.matmul_mx(
-                    out=banks[1][n if a == 0 else 2 + c][:, slot],
-                    lhsT=eye_w[:, slot].bitcast(FP8X4),
-                    lhsT_scale=eye_s[:, slot],
-                    rhs=wq_w[a][u][:, cols].bitcast(FP8X4),
-                    rhs_scale=wq_s[a][u][:, cols],
+                    out=scratch_bank(a, n)[:, part],
+                    lhsT=eye_w[:, part].bitcast(FP8X4),
+                    lhsT_scale=eye_s[:, part],
+                    rhs=wq_w[a, u][:, cols].bitcast(FP8X4),
+                    rhs_scale=wq_s[a, u][:, cols],
                     start=True,
                     stop=True,
                 )
-
-        def residual(a, n):
-            u, c = divmod(n, 2)
-            cols = slice(c * P, (c + 1) * P)
             nc.vector.tensor_tensor(
-                out=cols_view(wr_bf[a][u][:, cols, :]),
+                out=cols_view(wr_bf[a, u][:, cols, :]),
                 in0=rows_view(wt_raw[a][u][:, :, cols]),
-                in1=rows_view(banks[1][n if a == 0 else 2 + c][:].rearrange("p (i c) -> p i c", i=PACK)),
+                in1=rows_view(scratch_bank(a, n)[:].rearrange("p (i c) -> p i c", i=PACK)),
                 op=SUBTRACT,
             )
 
-        def gather_scales(h, slot):
-            pick_s[h] = tile([P, HALF], U8, f"pick_s{h}", slot)
-            nc.vector.tensor_copy(
-                out=pick_s[h][:],
-                in_=tab_s[:].bitcast(U8).indirect(offsets[:, h * HALF // 16 : (h + 1) * HALF // 16]),
-            )
+        def second_tier(a, u, slot=None):
+            wr_w[a, u] = tile([P, N // 2], U32, f"wr_w{a}{u}", slot)
+            quantize(wr_w[a, u][:], wr_s[a, u][:], wr_bf[a, u][:])
 
-        def gather_words(a, h, slot):
-            pick_w[a, h] = tile([P, HALF], U32, f"pick_w{a}{h}", slot)
-            nc.vector.tensor_copy(
-                out=pick_w[a, h][:],
-                in_=tab_w[a][:].bitcast(U32).indirect(offsets[:, h * HALF // 16 : (h + 1) * HALF // 16]),
-            )
+        def gather(picked, key, window, groups, name, slot):
+            lo, hi = GROUPS[groups[0]].start, GROUPS[groups[-1]].stop
+            dst = tile([P, hi - lo], window.dtype, name, slot)
+            nc.vector.tensor_copy(out=dst[:], in_=window.indirect(offsets[:, lo // 16 : hi // 16]))
+            for g in groups:
+                picked[key + (g,)] = dst[:, GROUPS[g].start - lo : GROUPS[g].stop - lo]
 
-        def tab_pass(words, scales, a, h, n, start, stop=False):
-            u, c = divmod(n, 2)
-            cols = slice(c * P, (c + 1) * P)
-            nc.tensor.matmul_mx(
-                out=banks[h][n][:],
-                lhsT=words[a][u][:, cols].bitcast(FP8X4),
-                lhsT_scale=scales[a][u][:, cols],
-                rhs=pick_w[a, h][:].bitcast(FP8X4),
-                rhs_scale=pick_s[h][4 * a :, :],
-                start=start,
-                stop=stop,
-            )
+        def gather_scales(groups, slot):
+            gather(pick_s, (), tab_s[:].bitcast(U8), groups, f"pick_s{groups[0]}", slot)
 
-        def q_passes(a, h, tiles=range(N_TILES)):
+        def gather_words(a, groups, slot=None):
+            gather(pick_w, (a,), tab_w[a][:].bitcast(U32), groups, f"pick_w{a}{groups[0]}", slot)
+
+        def table_passes(words, scales, a, g, tiles, first):
             for n in tiles:
-                tab_pass(wq_w, wq_s, a, h, n, a == 0)
-
-        def r_passes(a, h, tiles=range(N_TILES), stop=False):
-            for n in tiles:
-                tab_pass(wr_w, wr_s, a, h, n, False, stop)
-
-        def x_passes(a, h, tiles=range(N_TILES)):
-            for n in tiles:
-                x_pass(a, h, n)
-
-        def load_wx(a):
-            nc.sync.dma_start(out=wx_w[:, a, :], in_=wx_words[a].rearrange("p n i -> p (n i)").bitcast(I32))
-
-        def x_pass(a, h, n, start=False, stop=False, part=slice(0, HALF)):
-            cols = slice(n * P, (n + 1) * P)
-            nc.tensor.matmul_mx(
-                out=banks[h][n][:, part],
-                lhsT=wx_w[:, a, cols].bitcast(FP8X4),
-                lhsT_scale=wx_s[4 * a :, :].bitcast(U8)[:, cols],
-                rhs=xq_w[a, h][:, part].bitcast(FP8X4),
-                rhs_scale=xq_s[a][h][:, part],
-                start=start,
-                stop=stop,
-            )
-
-        def finish(engine, h, n):
-            if engine == "scalar":
-                nc.scalar.activation(out=result[h][:, n, :], in_=banks[h][n][:], func=IDENTITY, bias=bias[:, n : n + 1])
-            else:
-                nc.vector.tensor_scalar(
-                    out=result[h][:, n, :], in0=banks[h][n][:], scalar1=bias[:, n : n + 1], scalar2=None, op0=ADD
+                u, c = divmod(n, 2)
+                cols = slice(c * P, (c + 1) * P)
+                nc.tensor.matmul_mx(
+                    out=sums(g, n),
+                    lhsT=words[a, u][:, cols].bitcast(FP8X4),
+                    lhsT_scale=scales[a, u][:, cols],
+                    rhs=pick_w[a, g].bitcast(FP8X4),
+                    rhs_scale=pick_s[g,][4 * a :, :],
+                    start=first and opens_bank(g, n),
+                    stop=False,
                 )
-            nc.sync.dma_start(out=out[n * P : (n + 1) * P, h * HALF : (h + 1) * HALF], in_=result[h][:, n, :])
+
+        def q_passes(a, g, tiles=range(N_TILES)):
+            table_passes(wq_w, wq_s, a, g, tiles, a == 0)
+
+        def r_passes(a, g, tiles=range(N_TILES)):
+            table_passes(wr_w, wr_s, a, g, tiles, False)
+
+        def x_passes(a, g):
+            for n in range(N_TILES):
+                cols = slice(n * P, (n + 1) * P)
+                nc.tensor.matmul_mx(
+                    out=sums(g, n),
+                    lhsT=wx_w[a][:, cols].bitcast(FP8X4),
+                    lhsT_scale=wx_s[4 * a :, :].bitcast(U8)[:, cols],
+                    rhs=xq_w[a, g][:].bitcast(FP8X4),
+                    rhs_scale=xq_s[a, g][:],
+                    start=False,
+                    stop=a == PASSES - 1 and closes_bank(g, n),
+                )
+
+        def finish(g, engines, slot=None):
+            result[g] = tile([P, N_TILES, width(g)], F32, f"result{g}", slot)
+            per_bank = BANK // width(g)
+            for n, engine in enumerate(engines):
+                if engine == "scalar":
+                    nc.scalar.activation(
+                        out=result[g][:, n, :], in_=sums(g, n), func=IDENTITY, bias=bias[:, n : n + 1]
+                    )
+                else:
+                    nc.vector.tensor_scalar(
+                        out=result[g][:, n, :], in0=sums(g, n), scalar1=bias[:, n : n + 1], scalar2=None, op0=ADD
+                    )
+                if closes_bank(g, n):
+                    lo = n + 1 - per_bank
+                    nc.sync.dma_start(
+                        out=out[lo * P : (n + 1) * P, GROUPS[g]].rearrange("(n p) c -> p n c", p=P),
+                        in_=result[g][:, lo : n + 1, :],
+                    )
 
         nc.vector.memset(tab_s[:], 0)
         nc.sync.dma_start(offsets[:], offs)
         load_scales(tab_s, tab_scales)
         for u in range(2):
             load_rows(wt_raw[0][u], wt, 0, slice(u * N // 2, (u + 1) * N // 2))
-        load_tab(0)
+        load_words(tab_w[0], tab_words[0])
         load_rows(wt_second[:], wt, 1, slice(0, N))
-        with nc.allow_non_contiguous_dma(reason="one bias value for each partition and output tile"):
-            nc.sync.dma_start(out=bias[:], in_=b.rearrange("(n p) -> p n", p=P))
+        load_words(tab_w[1], tab_words[1])
         nc.vector.memset(wx_s[:], 0)
         load_scales(wx_s, wx_scales)
-        load_wx(0)
-        load_x(0, 0)
-        load_tab(1)
-        load_wx(1)
-        load_x(1, 0)
-        load_x(0, 1)
-        load_x(1, 1, 0, QUARTER)
-        load_x(1, 1, QUARTER, HALF)
+        load_words(wx_w[0], wx_words[0])
+        load_x(0, FIRST)
+        load_words(wx_w[1], wx_words[1])
+        load_x(1, FIRST)
+        with nc.allow_non_contiguous_dma(reason="one bias value for each partition and output tile"):
+            nc.sync.dma_start(out=bias[:], in_=b.rearrange("(n p) -> p n", p=P))
+        for g in (MIDDLE, LAST):
+            for a in range(PASSES):
+                load_x(a, g)
 
         nc.gpsimd.memset(eye[:], 0.0)
         nc.gpsimd.affine_select(
@@ -228,78 +257,59 @@ def tile_list_tiert_bias_kernel(
             cols = slice(2 * v * P, 2 * (v + 1) * P)
             quantize(eye_w[:, cols], eye_s[:, cols], eye_bf[v][:])
 
-        def first_tier(a, u, slot_bf, slot_w):
-            wt_bf[a, u] = tile([P, N // 2, PACK], BF16, f"wt_bf{a}{u}", slot_bf)
-            wq_w[a][u] = tile([P, N // 2], U32, f"wq_w{a}{u}", slot_w)
-            cast("scalar", wt_bf[a, u][:], wt_raw[a][u])
-            quantize(wq_w[a][u][:], wq_s[a][u][:], wt_bf[a, u][:])
-
-        def leftover(a, u, slot=None):
-            wr_bf[a][u] = tile([P, N // 2, PACK], BF16, f"wr_bf{a}{u}", slot)
-            for n in (2 * u, 2 * u + 1):
-                decode(a, n)
-                residual(a, n)
-
-        def second_tier(a, u, slot=None):
-            wr_w[a][u] = tile([P, N // 2], U32, f"wr_w{a}{u}", slot)
-            quantize(wr_w[a][u][:], wr_s[a][u][:], wr_bf[a][u][:])
-
-        gather_scales(0, "eye_bf0")
-        first_tier(0, 0, None, "eye_bf1")
-        gather_scales(1, "wt_bf00")
-        first_tier(0, 1, None, "tab_s")
+        gather_scales((FIRST,), "eye_bf0")
+        first_tier(0, 0, "eye_bf1")
+        gather_scales((MIDDLE, LAST), "wt_bf00")
         leftover(0, 0)
-        gather_words(0, 0, "wt_bf01")
+        first_tier(0, 1, "tab_s")
         leftover(0, 1)
-        q_passes(0, 0)
-        first_tier(1, 0, None, "wt_raw00")
+        gather_words(0, (FIRST,), "wt_bf01")
         second_tier(0, 0)
+        leftover(0, 2)
+        leftover(0, 3)
+        q_passes(0, FIRST)
+        r_passes(0, FIRST, (0, 1))
+        gather_words(0, (MIDDLE, LAST), "wr_bf00")
+        first_tier(1, 0)
         second_tier(0, 1)
-        first_tier(1, 1, None, "wr_bf00")
-        gather_words(0, 1, "wr_bf01")
-        r_passes(0, 0)
+        first_tier(1, 1)
+        gather_words(1, (FIRST,))
+        q_passes(0, MIDDLE)
         leftover(1, 0)
-        q_passes(0, 1, (0, 1))
-        r_passes(0, 1, (0, 1))
-        x00 = cast_x("scalar", 0, 0, 0, HALF, None)
-        xq_w[0, 0] = tile([P, HALF], U32, "xq_w00", "tab_w0")
-        quantize_x(*x00)
-        gather_words(1, 0, "x_raw00")
-        leftover(1, 1, "x_bf000")
-        x_passes(0, 0)
-        q_passes(1, 0)
-        q_passes(0, 1, (2, 3))
-        r_passes(0, 1, (2, 3))
-        second_tier(1, 0, "wt_raw1")
+        leftover(1, 1)
+        r_passes(0, FIRST, (2, 3))
+        r_passes(0, MIDDLE)
+        second_tier(1, 0)
+        leftover(1, 2)
+        leftover(1, 3)
+        q_passes(1, FIRST)
+        r_passes(1, FIRST, (0, 1))
+        q_passes(0, LAST)
+        r_passes(0, LAST)
+        gather_words(1, (MIDDLE,), "wt_raw1")
         second_tier(1, 1)
-        gather_words(1, 1, "wr_bf10")
-        r_passes(1, 0)
-        xq_w[1, 0] = tile([P, HALF], U32, "xq_w10", "tab_w1")
-        quantize_x(*cast_x("scalar", 1, 0, 0, HALF, None))
-        for n in range(N_TILES):
-            x_pass(1, 0, n, stop=True)
-
-        x01 = cast_x("scalar", 0, 1, 0, HALF, None)
-        result[0] = tile([P, N_TILES, HALF], F32, "result0", "x_raw01")
-        result[1] = tile([P, N_TILES, HALF], F32, "result1")
-        for n in range(N_TILES):
-            finish("scalar", 0, n)
-        xq_w[0, 1] = tile([P, HALF], U32, "xq_w01")
-        xq_w[1, 1] = tile([P, HALF], U32, "xq_w11")
-        x11a = cast_x("vector", 1, 1, 0, QUARTER, "x_bf100")
-        quantize_x(*x01)
-        quantize_x(*x11a)
-        x11b = cast_x("vector", 1, 1, QUARTER, HALF, "x_bf010")
-        quantize_x(*x11b)
-        q_passes(1, 1, (0, 1, 2))
-        r_passes(1, 1, (0,))
-        x_passes(0, 1)
-        for n in range(N_TILES):
-            x_pass(1, 1, n, part=slice(0, QUARTER))
-        for n in range(N_TILES):
-            x_pass(1, 1, n, stop=n == 0, part=slice(QUARTER, HALF))
-            if n == 3:
-                q_passes(1, 1, (n,))
-            if n > 0:
-                r_passes(1, 1, (n,), stop=True)
-            finish("scalar" if n % 2 == 1 else "vector", 1, n)
+        q_passes(1, MIDDLE)
+        r_passes(1, FIRST, (2, 3))
+        cast_x(0, FIRST, ("scalar",))
+        quantize_x(0, FIRST, "wr_bf11")
+        x_passes(0, FIRST)
+        r_passes(1, MIDDLE)
+        cast_x(1, FIRST, ("scalar", "vector"))
+        quantize_x(1, FIRST)
+        x_passes(1, FIRST)
+        gather_words(1, (LAST,), "x_bf10")
+        q_passes(1, LAST)
+        cast_x(0, MIDDLE, ("scalar",))
+        finish(FIRST, ("scalar",) * N_TILES, "x_raw01")
+        cast_x(1, MIDDLE, ("vector",))
+        quantize_x(0, MIDDLE)
+        quantize_x(1, MIDDLE)
+        x_passes(0, MIDDLE)
+        r_passes(1, LAST)
+        x_passes(1, MIDDLE)
+        finish(MIDDLE, ("scalar",) * N_TILES)
+        for a in range(PASSES):
+            cast_x(a, LAST, ("vector",))
+            quantize_x(a, LAST)
+            x_passes(a, LAST)
+        finish(LAST, ("scalar", "scalar", "vector", "vector"))

@@ -152,6 +152,18 @@ def tile_list_tiert_bias_kernel(
                 op=SUBTRACT,
             )
 
+        def warm_up(bank, words, scales, count):
+            for repeat in range(count):
+                nc.tensor.matmul_mx(
+                    out=banks[bank][:, : words.shape[1]],
+                    lhsT=eye_w[:, :P].bitcast(FP8X4),
+                    lhsT_scale=eye_s[:, :P],
+                    rhs=words.bitcast(FP8X4),
+                    rhs_scale=scales,
+                    start=True,
+                    stop=True,
+                )
+
         def second_tier(a, u, slot=None):
             wr_w[a, u] = tile([P, N // 2], U32, f"wr_w{a}{u}", slot)
             quantize(wr_w[a, u][:], wr_s[a, u][:], wr_bf[a, u][:])
@@ -202,9 +214,9 @@ def tile_list_tiert_bias_kernel(
                     stop=a == PASSES - 1 and closes_bank(g, n),
                 )
 
-        def finish(g, engines, slot=None):
+        def finish(g, engines, slot=None, tiles_a_store=None):
             result[g] = tile([P, N_TILES, width(g)], F32, f"result{g}", slot)
-            per_bank = BANK // width(g)
+            per_store = tiles_a_store or BANK // width(g)
             for n, engine in enumerate(engines):
                 if engine == "scalar":
                     nc.scalar.activation(
@@ -214,8 +226,8 @@ def tile_list_tiert_bias_kernel(
                     nc.vector.tensor_scalar(
                         out=result[g][:, n, :], in0=sums(g, n), scalar1=bias[:, n : n + 1], scalar2=None, op0=ADD
                     )
-                if closes_bank(g, n):
-                    lo = n + 1 - per_bank
+                if (n + 1) % per_store == 0:
+                    lo = n + 1 - per_store
                     nc.sync.dma_start(
                         out=out[lo * P : (n + 1) * P, GROUPS[g]].rearrange("(n p) c -> p n c", p=P),
                         in_=result[g][:, lo : n + 1, :],
@@ -258,58 +270,66 @@ def tile_list_tiert_bias_kernel(
             quantize(eye_w[:, cols], eye_s[:, cols], eye_bf[v][:])
 
         gather_scales((FIRST,), "eye_bf0")
+        warm_up(0, eye_w[:], eye_s[:], 2)
         first_tier(0, 0, "eye_bf1")
-        gather_scales((MIDDLE, LAST), "wt_bf00")
+        gather_scales((MIDDLE,), "wt_bf00")
         leftover(0, 0)
-        first_tier(0, 1, "tab_s")
+        first_tier(0, 1, "eye")
         leftover(0, 1)
         gather_words(0, (FIRST,), "wt_bf01")
         second_tier(0, 0)
         leftover(0, 2)
+        gather_words(0, (MIDDLE,), "wr_bf00")
         leftover(0, 3)
+        warm_up(1, wq_w[0, 1][:], wq_s[0, 1][:], 6)
         q_passes(0, FIRST)
         r_passes(0, FIRST, (0, 1))
-        gather_words(0, (MIDDLE, LAST), "wr_bf00")
+        q_passes(0, MIDDLE)
+        r_passes(0, MIDDLE, (0, 1))
         first_tier(1, 0)
         second_tier(0, 1)
         first_tier(1, 1)
         gather_words(1, (FIRST,))
-        q_passes(0, MIDDLE)
         leftover(1, 0)
         leftover(1, 1)
         r_passes(0, FIRST, (2, 3))
-        r_passes(0, MIDDLE)
+        r_passes(0, MIDDLE, (2, 3))
+        q_passes(1, FIRST)
+        gather_words(1, (MIDDLE,), "wt_bf11")
         second_tier(1, 0)
         leftover(1, 2)
         leftover(1, 3)
-        q_passes(1, FIRST)
         r_passes(1, FIRST, (0, 1))
+        q_passes(1, MIDDLE)
+        r_passes(1, MIDDLE, (0, 1))
+        cast_x(0, FIRST, ("scalar",))
+        quantize_x(0, FIRST, "wr_bf10")
+        second_tier(1, 1, "x_raw00")
+        x_passes(0, FIRST)
+        r_passes(1, FIRST, (2, 3))
+        r_passes(1, MIDDLE, (2, 3))
+        gather_scales((LAST,), "x_bf00")
+        gather_words(0, (LAST,), "wr_bf11")
         q_passes(0, LAST)
         r_passes(0, LAST)
-        gather_words(1, (MIDDLE,), "wt_raw1")
-        second_tier(1, 1)
-        q_passes(1, MIDDLE)
-        r_passes(1, FIRST, (2, 3))
-        cast_x(0, FIRST, ("scalar",))
-        quantize_x(0, FIRST, "wr_bf11")
-        x_passes(0, FIRST)
-        r_passes(1, MIDDLE)
-        cast_x(1, FIRST, ("scalar", "vector"))
+        cast_x(1, FIRST, ("scalar",))
+        cast_x(0, MIDDLE, ("vector",))
         quantize_x(1, FIRST)
         x_passes(1, FIRST)
         gather_words(1, (LAST,), "x_bf10")
         q_passes(1, LAST)
-        cast_x(0, MIDDLE, ("scalar",))
-        finish(FIRST, ("scalar",) * N_TILES, "x_raw01")
-        cast_x(1, MIDDLE, ("vector",))
+        cast_x(1, MIDDLE, ("scalar",))
+        finish(FIRST, ("scalar",) * N_TILES, "x_raw11")
         quantize_x(0, MIDDLE)
+        cast_x(0, LAST, ("vector",))
         quantize_x(1, MIDDLE)
+        quantize_x(0, LAST)
         x_passes(0, MIDDLE)
-        r_passes(1, LAST)
         x_passes(1, MIDDLE)
+        r_passes(1, LAST)
+        x_passes(0, LAST)
         finish(MIDDLE, ("scalar",) * N_TILES)
-        for a in range(PASSES):
-            cast_x(a, LAST, ("vector",))
-            quantize_x(a, LAST)
-            x_passes(a, LAST)
-        finish(LAST, ("scalar", "scalar", "vector", "vector"))
+        cast_x(1, LAST, ("vector",))
+        quantize_x(1, LAST)
+        x_passes(1, LAST)
+        finish(LAST, ("scalar", "scalar", "vector", "vector"), None, 1)

@@ -65,6 +65,8 @@ def tile_list_tiert_bias_kernel(
         wx_s = tile([P, N // 4], I32, "wx_s")
         wx_w = [tile([P, N], I32, f"wx_w{a}") for a in range(PASSES)]
         bias = tile([P, N_TILES], F32, "bias")
+        bias_rows = tile([P, P], F32, "bias_rows")
+        unit = tile([P, P], F32, "unit")
         wt_first = [tile([P, PACK, N // 2], F32, f"wt_raw0{u}") for u in range(2)]
         wt_second = tile([P, PACK, N], F32, "wt_raw1")
         wt_raw = [[t[:] for t in wt_first], [wt_second[:, :, u * N // 2 : (u + 1) * N // 2] for u in range(2)]]
@@ -73,7 +75,10 @@ def tile_list_tiert_bias_kernel(
         wr_bf = {}
         wr_w = {}
         wr_s = {(a, u): tile([P, N // 2], U8, f"wr_s{a}{u}") for a in range(PASSES) for u in range(2)}
-        x_raw = {(a, g): tile([P, PACK, width(g)], F32, f"x_raw{a}{g}") for a in range(PASSES) for g in range(3)}
+        x_raw = {(a, g): tile([P, PACK, width(g)], F32, f"x_raw{a}{g}")[:] for a, g in ((0, 0), (1, 0), (1, 1), (1, 2))}
+        x_later = tile([P, PACK, J - width(FIRST)], F32, "x_later")
+        x_raw[0, MIDDLE] = x_later[:, :, : width(MIDDLE)]
+        x_raw[0, LAST] = x_later[:, :, width(MIDDLE) :]
         x_bf = {}
         xq_w = {}
         xq_s = {(a, g): tile([P, width(g)], U8, f"xq_s{a}{g}") for a in range(PASSES) for g in range(3)}
@@ -92,7 +97,7 @@ def tile_list_tiert_bias_kernel(
             nc.sync.dma_start(out=dst, in_=rows.rearrange("(p i) c -> p i c", i=PACK))
 
         def load_x(a, g):
-            load_rows(x_raw[a, g][:], x, a, GROUPS[g])
+            load_rows(x_raw[a, g], x, a, GROUPS[g])
 
         def load_words(dst, src):
             nc.sync.dma_start(out=dst[:], in_=src.rearrange("p t i -> p (t i)").bitcast(I32))
@@ -123,8 +128,8 @@ def tile_list_tiert_bias_kernel(
             xq_w[a, g] = tile([P, width(g)], U32, f"xq_w{a}{g}", slot)
             quantize(xq_w[a, g][:], xq_s[a, g][:], x_bf[a, g][:])
 
-        def first_tier(a, u, slot=None):
-            wt_bf = tile([P, N // 2, PACK], BF16, f"wt_bf{a}{u}")
+        def first_tier(a, u, slot=None, cast_slot=None):
+            wt_bf = tile([P, N // 2, PACK], BF16, f"wt_bf{a}{u}", cast_slot)
             wq_w[a, u] = tile([P, N // 2], U32, f"wq_w{a}{u}", slot)
             cast("scalar", wt_bf[:], wt_raw[a][u])
             quantize(wq_w[a, u][:], wq_s[a, u][:], wt_bf[:])
@@ -236,8 +241,10 @@ def tile_list_tiert_bias_kernel(
         nc.vector.memset(tab_s[:], 0)
         nc.sync.dma_start(offsets[:], offs)
         load_scales(tab_s, tab_scales)
-        for u in range(2):
-            load_rows(wt_raw[0][u], wt, 0, slice(u * N // 2, (u + 1) * N // 2))
+        load_rows(wt_raw[0][0], wt, 0, slice(0, N // 2))
+        nc.vector.memset(bias_rows[:], 0.0)
+        nc.sync.dma_start(out=bias_rows[:N_TILES, :], in_=b.rearrange("(n p) -> n p", p=P))
+        load_rows(wt_raw[0][1], wt, 0, slice(N // 2, N))
         load_words(tab_w[0], tab_words[0])
         load_rows(wt_second[:], wt, 1, slice(0, N))
         load_words(tab_w[1], tab_words[1])
@@ -247,11 +254,9 @@ def tile_list_tiert_bias_kernel(
         load_x(0, FIRST)
         load_words(wx_w[1], wx_words[1])
         load_x(1, FIRST)
-        with nc.allow_non_contiguous_dma(reason="one bias value for each partition and output tile"):
-            nc.sync.dma_start(out=bias[:], in_=b.rearrange("(n p) -> p n", p=P))
-        for g in (MIDDLE, LAST):
-            for a in range(PASSES):
-                load_x(a, g)
+        load_rows(x_later[:], x, 0, slice(width(FIRST), J))
+        load_x(1, MIDDLE)
+        load_x(1, LAST)
 
         nc.gpsimd.memset(eye[:], 0.0)
         nc.gpsimd.affine_select(
@@ -269,6 +274,7 @@ def tile_list_tiert_bias_kernel(
             cols = slice(2 * v * P, 2 * (v + 1) * P)
             quantize(eye_w[:, cols], eye_s[:, cols], eye_bf[v][:])
 
+        nc.vector.tensor_copy(out=unit[:], in_=eye[:, PACK - 1 : K_PASS : PACK])
         gather_scales((FIRST,), "eye_bf0")
         warm_up(0, eye_w[:], eye_s[:], 2)
         first_tier(0, 0, "eye_bf1")
@@ -276,6 +282,8 @@ def tile_list_tiert_bias_kernel(
         leftover(0, 0)
         first_tier(0, 1, "eye")
         leftover(0, 1)
+        nc.tensor.transpose(banks[3][:, :P], bias_rows[:], unit[:])
+        nc.scalar.activation(out=bias[:], in_=banks[3][:, :N_TILES], func=IDENTITY)
         gather_words(0, (FIRST,), "wt_bf01")
         second_tier(0, 0)
         leftover(0, 2)
@@ -288,14 +296,14 @@ def tile_list_tiert_bias_kernel(
         r_passes(0, MIDDLE, (0, 1))
         first_tier(1, 0)
         second_tier(0, 1)
-        first_tier(1, 1)
         gather_words(1, (FIRST,))
+        first_tier(1, 1, None, "wt_bf10")
         leftover(1, 0)
         leftover(1, 1)
         r_passes(0, FIRST, (2, 3))
         r_passes(0, MIDDLE, (2, 3))
         q_passes(1, FIRST)
-        gather_words(1, (MIDDLE,), "wt_bf11")
+        gather_words(1, (MIDDLE,), "wt_bf10")
         second_tier(1, 0)
         leftover(1, 2)
         leftover(1, 3)
@@ -313,16 +321,16 @@ def tile_list_tiert_bias_kernel(
         q_passes(0, LAST)
         r_passes(0, LAST)
         cast_x(1, FIRST, ("scalar",))
-        cast_x(0, MIDDLE, ("vector",))
+        cast_x(0, MIDDLE, ("scalar",))
         quantize_x(1, FIRST)
         x_passes(1, FIRST)
         gather_words(1, (LAST,), "x_bf10")
         q_passes(1, LAST)
-        cast_x(1, MIDDLE, ("scalar",))
-        finish(FIRST, ("scalar",) * N_TILES, "x_raw11")
+        finish(FIRST, ("scalar",) * N_TILES)
+        cast_x(1, MIDDLE, ("vector",), "tab_w1")
         quantize_x(0, MIDDLE)
-        cast_x(0, LAST, ("vector",))
         quantize_x(1, MIDDLE)
+        cast_x(0, LAST, ("vector",), "x_bf01")
         quantize_x(0, LAST)
         x_passes(0, MIDDLE)
         x_passes(1, MIDDLE)

@@ -21,10 +21,16 @@ PACK = 4
 K_PASS = P * PACK
 PASSES = K // K_PASS
 N_TILES = N // P
+PAIR = 2 * P
+LOW_TILES, HIGH_TILES = (0, 1), (2, 3)
 BANK = 512
+BANKS = 8
+QUADRANT = 32
+LIST_ROWS = 16
 RUN = 4
+
 GROUPS = (slice(0, 512), slice(512, 768), slice(768, 1024))
-FIRST, MIDDLE, LAST = range(3)
+FIRST, MIDDLE, LAST = range(len(GROUPS))
 
 
 def tile_list_tiert_bias_kernel(
@@ -35,18 +41,17 @@ def tile_list_tiert_bias_kernel(
         sb = ctx.enter_context(tc.tile_pool(name="sb", bufs=1))
         psum = ctx.enter_context(tc.psum_pool(name="psum", bufs=1))
 
-        def tile(shape, dtype, name, slot=None):
-            return sb.tile(shape, dtype, name=name, tag=slot or name, align_bytes=64)
+        def tile(shape, dtype, name, after=None):
+            return sb.tile(shape, dtype, name=name, tag=after or name, align_bytes=64)
 
         def width(g):
             return GROUPS[g].stop - GROUPS[g].start
 
-        offsets = sb.tile([P, J // 16], U16, name="offsets")
-        banks = [psum.tile([P, BANK], F32, name=f"bank{i}") for i in range(8)]
+        offsets = sb.tile([P, J // LIST_ROWS], U16, name="offsets")
+        banks = [psum.tile([P, BANK], F32, name=f"bank{i}") for i in range(BANKS)]
 
         def sums(g, n):
-            first = GROUPS[g].start * N_TILES + n * width(g)
-            bank, col = divmod(first, BANK)
+            bank, col = divmod(GROUPS[g].start * N_TILES + n * width(g), BANK)
             return banks[bank][:, col : col + width(g)]
 
         def opens_bank(g, n):
@@ -55,8 +60,8 @@ def tile_list_tiert_bias_kernel(
         def closes_bank(g, n):
             return (n + 1) * width(g) % BANK == 0
 
-        def scratch_bank(a, n):
-            return banks[4 + n if a == 0 else 6 + n % 2]
+        def borrowed_bank(a, n):
+            return banks[BANKS // 2 + n] if a == 0 else banks[BANKS - 2 + n % 2]
 
         tab_s = tile([P, T // 4], I32, "tab_s")
         tab_w = [tile([P, T], I32, f"tab_w{a}") for a in range(PASSES)]
@@ -67,30 +72,35 @@ def tile_list_tiert_bias_kernel(
         bias = tile([P, N_TILES], F32, "bias")
         bias_rows = tile([P, P], F32, "bias_rows")
         unit = tile([P, P], F32, "unit")
-        wt_first = [tile([P, PACK, N // 2], F32, f"wt_raw0{u}") for u in range(2)]
+        wt_first = [tile([P, PACK, PAIR], F32, f"wt_raw0{u}") for u in range(2)]
         wt_second = tile([P, PACK, N], F32, "wt_raw1")
-        wt_raw = [[t[:] for t in wt_first], [wt_second[:, :, u * N // 2 : (u + 1) * N // 2] for u in range(2)]]
+        wt_raw = [[t[:] for t in wt_first], [wt_second[:, :, u * PAIR : (u + 1) * PAIR] for u in range(2)]]
         wq_w = {}
-        wq_s = {(a, u): tile([P, N // 2], U8, f"wq_s{a}{u}") for a in range(PASSES) for u in range(2)}
+        wq_s = {(a, u): tile([P, PAIR], U8, f"wq_s{a}{u}") for a in range(PASSES) for u in range(2)}
         wr_bf = {}
         wr_w = {}
-        wr_s = {(a, u): tile([P, N // 2], U8, f"wr_s{a}{u}") for a in range(PASSES) for u in range(2)}
-        x_raw = {(a, g): tile([P, PACK, width(g)], F32, f"x_raw{a}{g}")[:] for a, g in ((0, 0), (1, 0), (1, 1), (1, 2))}
+        wr_s = {(a, u): tile([P, PAIR], U8, f"wr_s{a}{u}") for a in range(PASSES) for u in range(2)}
+        x_raw = {
+            (a, g): tile([P, PACK, width(g)], F32, f"x_raw{a}{g}")[:]
+            for a, g in ((0, FIRST), (1, FIRST), (1, MIDDLE), (1, LAST))
+        }
         x_later = tile([P, PACK, J - width(FIRST)], F32, "x_later")
         x_raw[0, MIDDLE] = x_later[:, :, : width(MIDDLE)]
         x_raw[0, LAST] = x_later[:, :, width(MIDDLE) :]
         x_bf = {}
         xq_w = {}
-        xq_s = {(a, g): tile([P, width(g)], U8, f"xq_s{a}{g}") for a in range(PASSES) for g in range(3)}
-        result = {}
-        eye = tile([P, K_PASS + PACK], BF16, "eye")
+        xq_s = {(a, g): tile([P, width(g)], U8, f"xq_s{a}{g}") for a in range(PASSES) for g in range(len(GROUPS))}
+        ones = tile([P, K_PASS + PACK], BF16, "ones")
         eye_bf = [tile([P, 2, K_PASS], BF16, f"eye_bf{v}") for v in range(2)]
         eye_w = tile([P, PACK * P], U32, "eye_w")
         eye_s = tile([P, PACK * P], U8, "eye_s")
 
         def load_scales(dst, src):
-            for q in range(4):
-                nc.sync.dma_start(out=dst[32 * q : 32 * q + 8, :], in_=src[:, 4 * q : 4 * q + 4, :].bitcast(I32))
+            for q in range(P // QUADRANT):
+                nc.sync.dma_start(
+                    out=dst[QUADRANT * q : QUADRANT * q + 4 * PASSES, :],
+                    in_=src[:, 4 * q : 4 * q + 4, :].bitcast(I32),
+                )
 
         def load_rows(dst, src, a, cols):
             rows = src[a * K_PASS : (a + 1) * K_PASS, cols]
@@ -117,32 +127,29 @@ def tile_list_tiert_bias_kernel(
         def quantize(words, scales, src):
             nc.vector.quantize_mx(out=words.bitcast(FP8X4), scales=scales, in_=src.rearrange("p c i -> p (c i)"))
 
-        def cast_x(a, g, engines, slot=None):
-            x_bf[a, g] = tile([P, width(g), PACK], BF16, f"x_bf{a}{g}", slot)
-            share = width(g) // len(engines)
-            for s, engine in enumerate(engines):
-                cols = slice(s * share, (s + 1) * share)
-                cast(engine, x_bf[a, g][:, cols, :], x_raw[a, g][:, :, cols])
+        def cast_x(a, g, engine, after=None):
+            x_bf[a, g] = tile([P, width(g), PACK], BF16, f"x_bf{a}{g}", after)
+            cast(engine, x_bf[a, g][:], x_raw[a, g])
 
-        def quantize_x(a, g, slot=None):
-            xq_w[a, g] = tile([P, width(g)], U32, f"xq_w{a}{g}", slot)
+        def quantize_x(a, g, after=None):
+            xq_w[a, g] = tile([P, width(g)], U32, f"xq_w{a}{g}", after)
             quantize(xq_w[a, g][:], xq_s[a, g][:], x_bf[a, g][:])
 
-        def first_tier(a, u, slot=None, cast_slot=None):
-            wt_bf = tile([P, N // 2, PACK], BF16, f"wt_bf{a}{u}", cast_slot)
-            wq_w[a, u] = tile([P, N // 2], U32, f"wq_w{a}{u}", slot)
+        def first_tier(a, u, after=None, cast_after=None):
+            wt_bf = tile([P, PAIR, PACK], BF16, f"wt_bf{a}{u}", cast_after)
+            wq_w[a, u] = tile([P, PAIR], U32, f"wq_w{a}{u}", after)
             cast("scalar", wt_bf[:], wt_raw[a][u])
             quantize(wq_w[a, u][:], wq_s[a, u][:], wt_bf[:])
 
-        def leftover(a, n, slot=None):
+        def leftover(a, n):
             u, c = divmod(n, 2)
             cols = slice(c * P, (c + 1) * P)
             if c == 0:
-                wr_bf[a, u] = tile([P, N // 2, PACK], BF16, f"wr_bf{a}{u}", slot)
+                wr_bf[a, u] = tile([P, PAIR, PACK], BF16, f"wr_bf{a}{u}")
             for i in range(PACK):
                 part = slice(i * P, (i + 1) * P)
                 nc.tensor.matmul_mx(
-                    out=scratch_bank(a, n)[:, part],
+                    out=borrowed_bank(a, n)[:, part],
                     lhsT=eye_w[:, part].bitcast(FP8X4),
                     lhsT_scale=eye_s[:, part],
                     rhs=wq_w[a, u][:, cols].bitcast(FP8X4),
@@ -153,38 +160,25 @@ def tile_list_tiert_bias_kernel(
             nc.vector.tensor_tensor(
                 out=cols_view(wr_bf[a, u][:, cols, :]),
                 in0=rows_view(wt_raw[a][u][:, :, cols]),
-                in1=rows_view(scratch_bank(a, n)[:].rearrange("p (i c) -> p i c", i=PACK)),
+                in1=rows_view(borrowed_bank(a, n)[:].rearrange("p (i c) -> p i c", i=PACK)),
                 op=SUBTRACT,
             )
 
-        def warm_up(bank, words, scales, count):
-            for repeat in range(count):
-                nc.tensor.matmul_mx(
-                    out=banks[bank][:, : words.shape[1]],
-                    lhsT=eye_w[:, :P].bitcast(FP8X4),
-                    lhsT_scale=eye_s[:, :P],
-                    rhs=words.bitcast(FP8X4),
-                    rhs_scale=scales,
-                    start=True,
-                    stop=True,
-                )
-
-        def second_tier(a, u, slot=None):
-            wr_w[a, u] = tile([P, N // 2], U32, f"wr_w{a}{u}", slot)
+        def second_tier(a, u, after=None):
+            wr_w[a, u] = tile([P, PAIR], U32, f"wr_w{a}{u}", after)
             quantize(wr_w[a, u][:], wr_s[a, u][:], wr_bf[a, u][:])
 
-        def gather(picked, key, window, groups, name, slot):
-            lo, hi = GROUPS[groups[0]].start, GROUPS[groups[-1]].stop
-            dst = tile([P, hi - lo], window.dtype, name, slot)
-            nc.vector.tensor_copy(out=dst[:], in_=window.indirect(offsets[:, lo // 16 : hi // 16]))
-            for g in groups:
-                picked[key + (g,)] = dst[:, GROUPS[g].start - lo : GROUPS[g].stop - lo]
+        def gather(window, g, name, after):
+            dst = tile([P, width(g)], window.dtype, name, after)
+            entries = offsets[:, GROUPS[g].start // LIST_ROWS : GROUPS[g].stop // LIST_ROWS]
+            nc.vector.tensor_copy(out=dst[:], in_=window.indirect(entries))
+            return dst
 
-        def gather_scales(groups, slot):
-            gather(pick_s, (), tab_s[:].bitcast(U8), groups, f"pick_s{groups[0]}", slot)
+        def gather_scales(g, after):
+            pick_s[g] = gather(tab_s[:].bitcast(U8), g, f"pick_s{g}", after)
 
-        def gather_words(a, groups, slot=None):
-            gather(pick_w, (a,), tab_w[a][:].bitcast(U32), groups, f"pick_w{a}{groups[0]}", slot)
+        def gather_words(a, g, after=None):
+            pick_w[a, g] = gather(tab_w[a][:].bitcast(U32), g, f"pick_w{a}{g}", after)
 
         def table_passes(words, scales, a, g, tiles, first):
             for n in tiles:
@@ -194,14 +188,14 @@ def tile_list_tiert_bias_kernel(
                     out=sums(g, n),
                     lhsT=words[a, u][:, cols].bitcast(FP8X4),
                     lhsT_scale=scales[a, u][:, cols],
-                    rhs=pick_w[a, g].bitcast(FP8X4),
-                    rhs_scale=pick_s[g,][4 * a :, :],
+                    rhs=pick_w[a, g][:].bitcast(FP8X4),
+                    rhs_scale=pick_s[g][4 * a :, :],
                     start=first and opens_bank(g, n),
                     stop=False,
                 )
 
-        def q_passes(a, g, tiles=range(N_TILES)):
-            table_passes(wq_w, wq_s, a, g, tiles, a == 0)
+        def q_passes(a, g):
+            table_passes(wq_w, wq_s, a, g, range(N_TILES), a == 0)
 
         def r_passes(a, g, tiles=range(N_TILES)):
             table_passes(wr_w, wr_s, a, g, tiles, False)
@@ -219,32 +213,29 @@ def tile_list_tiert_bias_kernel(
                     stop=a == PASSES - 1 and closes_bank(g, n),
                 )
 
-        def finish(g, engines, slot=None, tiles_a_store=None):
-            result[g] = tile([P, N_TILES, width(g)], F32, f"result{g}", slot)
-            per_store = tiles_a_store or BANK // width(g)
+        def finish(g, engines, tiles_a_store):
+            result = tile([P, N_TILES, width(g)], F32, f"result{g}")
             for n, engine in enumerate(engines):
                 if engine == "scalar":
-                    nc.scalar.activation(
-                        out=result[g][:, n, :], in_=sums(g, n), func=IDENTITY, bias=bias[:, n : n + 1]
-                    )
+                    nc.scalar.activation(out=result[:, n, :], in_=sums(g, n), func=IDENTITY, bias=bias[:, n : n + 1])
                 else:
                     nc.vector.tensor_scalar(
-                        out=result[g][:, n, :], in0=sums(g, n), scalar1=bias[:, n : n + 1], scalar2=None, op0=ADD
+                        out=result[:, n, :], in0=sums(g, n), scalar1=bias[:, n : n + 1], scalar2=None, op0=ADD
                     )
-                if (n + 1) % per_store == 0:
-                    lo = n + 1 - per_store
+                if (n + 1) % tiles_a_store == 0:
+                    lo = n + 1 - tiles_a_store
                     nc.sync.dma_start(
                         out=out[lo * P : (n + 1) * P, GROUPS[g]].rearrange("(n p) c -> p n c", p=P),
-                        in_=result[g][:, lo : n + 1, :],
+                        in_=result[:, lo : n + 1, :],
                     )
 
         nc.vector.memset(tab_s[:], 0)
         nc.sync.dma_start(offsets[:], offs)
         load_scales(tab_s, tab_scales)
-        load_rows(wt_raw[0][0], wt, 0, slice(0, N // 2))
+        load_rows(wt_raw[0][0], wt, 0, slice(0, PAIR))
         nc.vector.memset(bias_rows[:], 0.0)
         nc.sync.dma_start(out=bias_rows[:N_TILES, :], in_=b.rearrange("(n p) -> n p", p=P))
-        load_rows(wt_raw[0][1], wt, 0, slice(N // 2, N))
+        load_rows(wt_raw[0][1], wt, 0, slice(PAIR, N))
         load_words(tab_w[0], tab_words[0])
         load_rows(wt_second[:], wt, 1, slice(0, N))
         load_words(tab_w[1], tab_words[1])
@@ -252,16 +243,16 @@ def tile_list_tiert_bias_kernel(
         load_scales(wx_s, wx_scales)
         load_words(wx_w[0], wx_words[0])
         load_x(0, FIRST)
-        load_words(wx_w[1], wx_words[1])
         load_x(1, FIRST)
+        load_words(wx_w[1], wx_words[1])
         load_rows(x_later[:], x, 0, slice(width(FIRST), J))
         load_x(1, MIDDLE)
         load_x(1, LAST)
 
-        nc.gpsimd.memset(eye[:], 0.0)
+        nc.gpsimd.memset(ones[:], 0.0)
         nc.gpsimd.affine_select(
-            out=eye[:],
-            in_=eye[:],
+            out=ones[:],
+            in_=ones[:],
             compare_op=mybir.AluOpType.not_equal,
             fill=1.0,
             base=PACK - 1,
@@ -269,75 +260,75 @@ def tile_list_tiert_bias_kernel(
             channel_multiplier=PACK,
         )
         for i in range(PACK):
-            nc.vector.tensor_copy(out=eye_bf[i // 2][:, i % 2, :], in_=eye[:, PACK - 1 - i : PACK - 1 - i + K_PASS])
+            nc.vector.tensor_copy(out=eye_bf[i // 2][:, i % 2, :], in_=ones[:, PACK - 1 - i : PACK - 1 - i + K_PASS])
         for v in range(2):
             cols = slice(2 * v * P, 2 * (v + 1) * P)
             quantize(eye_w[:, cols], eye_s[:, cols], eye_bf[v][:])
+        nc.vector.tensor_copy(out=unit[:], in_=ones[:, PACK - 1 : K_PASS : PACK])
 
-        nc.vector.tensor_copy(out=unit[:], in_=eye[:, PACK - 1 : K_PASS : PACK])
-        gather_scales((FIRST,), "eye_bf0")
-        warm_up(0, eye_w[:], eye_s[:], 2)
-        first_tier(0, 0, "eye_bf1")
-        gather_scales((MIDDLE,), "wt_bf00")
+        gather_scales(FIRST, after="eye_bf0")
+        first_tier(0, 0, after="eye_bf1")
+        gather_scales(MIDDLE, after="wt_bf00")
         leftover(0, 0)
-        first_tier(0, 1, "eye")
+        first_tier(0, 1, after="ones")
         leftover(0, 1)
-        nc.tensor.transpose(banks[3][:, :P], bias_rows[:], unit[:])
-        nc.scalar.activation(out=bias[:], in_=banks[3][:, :N_TILES], func=IDENTITY)
-        gather_words(0, (FIRST,), "wt_bf01")
+        nc.tensor.transpose(sums(FIRST, N_TILES - 1)[:, :P], bias_rows[:], unit[:])
+        nc.scalar.activation(out=bias[:], in_=sums(FIRST, N_TILES - 1)[:, :N_TILES], func=IDENTITY)
+        gather_words(0, FIRST, after="wt_bf01")
         second_tier(0, 0)
         leftover(0, 2)
-        gather_words(0, (MIDDLE,), "wr_bf00")
+        gather_words(0, MIDDLE, after="wr_bf00")
         leftover(0, 3)
-        warm_up(1, wq_w[0, 1][:], wq_s[0, 1][:], 6)
-        q_passes(0, FIRST)
-        r_passes(0, FIRST, (0, 1))
-        q_passes(0, MIDDLE)
-        r_passes(0, MIDDLE, (0, 1))
+        for g in (FIRST, MIDDLE):
+            q_passes(0, g)
+            r_passes(0, g, LOW_TILES)
+
         first_tier(1, 0)
         second_tier(0, 1)
-        gather_words(1, (FIRST,))
-        first_tier(1, 1, None, "wt_bf10")
+        gather_words(1, FIRST)
+        first_tier(1, 1, cast_after="wt_bf10")
         leftover(1, 0)
         leftover(1, 1)
-        r_passes(0, FIRST, (2, 3))
-        r_passes(0, MIDDLE, (2, 3))
+        r_passes(0, FIRST, HIGH_TILES)
+        r_passes(0, MIDDLE, HIGH_TILES)
         q_passes(1, FIRST)
-        gather_words(1, (MIDDLE,), "wt_bf10")
+        gather_words(1, MIDDLE, after="wt_bf10")
         second_tier(1, 0)
         leftover(1, 2)
         leftover(1, 3)
-        r_passes(1, FIRST, (0, 1))
+        r_passes(1, FIRST, LOW_TILES)
         q_passes(1, MIDDLE)
-        r_passes(1, MIDDLE, (0, 1))
-        cast_x(0, FIRST, ("scalar",))
-        quantize_x(0, FIRST, "wr_bf10")
-        second_tier(1, 1, "x_raw00")
+        r_passes(1, MIDDLE, LOW_TILES)
+        cast_x(0, FIRST, "scalar")
+        quantize_x(0, FIRST, after="wr_bf10")
+        second_tier(1, 1, after="x_raw00")
         x_passes(0, FIRST)
-        r_passes(1, FIRST, (2, 3))
-        r_passes(1, MIDDLE, (2, 3))
-        gather_scales((LAST,), "x_bf00")
-        gather_words(0, (LAST,), "wr_bf11")
+        r_passes(1, FIRST, HIGH_TILES)
+        r_passes(1, MIDDLE, HIGH_TILES)
+
+        gather_scales(LAST, after="x_bf00")
+        gather_words(0, LAST, after="wr_bf11")
         q_passes(0, LAST)
         r_passes(0, LAST)
-        cast_x(1, FIRST, ("scalar",))
-        cast_x(0, MIDDLE, ("scalar",))
+        cast_x(1, FIRST, "scalar")
+        cast_x(0, MIDDLE, "scalar")
         quantize_x(1, FIRST)
         x_passes(1, FIRST)
-        gather_words(1, (LAST,), "x_bf10")
+        gather_words(1, LAST, after="x_bf10")
         q_passes(1, LAST)
-        finish(FIRST, ("scalar",) * N_TILES)
-        cast_x(1, MIDDLE, ("vector",), "tab_w1")
+
+        finish(FIRST, ("scalar",) * N_TILES, tiles_a_store=1)
+        cast_x(1, MIDDLE, "vector", after="tab_w1")
         quantize_x(0, MIDDLE)
         quantize_x(1, MIDDLE)
-        cast_x(0, LAST, ("vector",), "x_bf01")
+        cast_x(0, LAST, "vector", after="x_bf01")
         quantize_x(0, LAST)
         x_passes(0, MIDDLE)
         x_passes(1, MIDDLE)
         r_passes(1, LAST)
         x_passes(0, LAST)
-        finish(MIDDLE, ("scalar",) * N_TILES)
-        cast_x(1, LAST, ("vector",))
+        finish(MIDDLE, ("scalar",) * N_TILES, tiles_a_store=2)
+        cast_x(1, LAST, "vector")
         quantize_x(1, LAST)
         x_passes(1, LAST)
-        finish(LAST, ("scalar", "scalar", "vector", "vector"), None, 1)
+        finish(LAST, ("scalar", "scalar", "vector", "vector"), tiles_a_store=1)

@@ -16,6 +16,8 @@ IDENTITY = mybir.ActivationFunctionType.Identity
 SUBTRACT = mybir.AluOpType.subtract
 ADD = mybir.AluOpType.add
 
+ELEMENT_BYTES = ((F32, 4), (I32, 4), (U32, 4), (BF16, 2), (U8, 1))
+ALIGN = 64
 P = 128
 PACK = 4
 K_PASS = P * PACK
@@ -39,10 +41,22 @@ def tile_list_tiert_bias_kernel(
     nc = tc.nc
     with ExitStack() as ctx:
         sb = ctx.enter_context(tc.tile_pool(name="sb", bufs=1))
+        arena = ctx.enter_context(tc.tile_pool(name="arena", bufs=1))
         psum = ctx.enter_context(tc.psum_pool(name="psum", bufs=1))
+        place = {"end": 0}
 
-        def tile(shape, dtype, name, after=None):
-            return sb.tile(shape, dtype, name=name, tag=after or name, align_bytes=64)
+        def tile(shape, dtype, name, after=None, pad=0):
+            if after is None:
+                place[name] = place["end"] + pad
+                size = [n for t, n in ELEMENT_BYTES if t == dtype][0]
+                for n in shape[1:]:
+                    size = size * n
+                place["end"] = place["end"] + 2 * pad + -(-size // ALIGN) * ALIGN
+            elif isinstance(after, tuple):
+                place[name] = place[after[0]] + after[1]
+            else:
+                place[name] = place[after]
+            return arena.tile(shape, dtype, name=name, offset=place[name], align_bytes=ALIGN)
 
         def width(g):
             return GROUPS[g].stop - GROUPS[g].start
@@ -75,18 +89,18 @@ def tile_list_tiert_bias_kernel(
         wt_first = [tile([P, PACK, PAIR], F32, f"wt_raw0{u}") for u in range(2)]
         wt_second = tile([P, PACK, N], F32, "wt_raw1")
         wt_raw = [[t[:] for t in wt_first], [wt_second[:, :, u * PAIR : (u + 1) * PAIR] for u in range(2)]]
+        wt_bf = {}
         wq_w = {}
         wq_s = {(a, u): tile([P, PAIR], U8, f"wq_s{a}{u}") for a in range(PASSES) for u in range(2)}
+        decoded = {}
         wr_bf = {}
         wr_w = {}
         wr_s = {(a, u): tile([P, PAIR], U8, f"wr_s{a}{u}") for a in range(PASSES) for u in range(2)}
         x_raw = {
-            (a, g): tile([P, PACK, width(g)], F32, f"x_raw{a}{g}")[:]
-            for a, g in ((0, FIRST), (1, FIRST), (1, MIDDLE), (1, LAST))
+            (a, g): tile([P, PACK, width(g)], F32, f"x_raw{a}{g}", pad=4096 if (a, g) == (0, MIDDLE) else 0)[:]
+            for a in range(PASSES)
+            for g in range(len(GROUPS))
         }
-        x_later = tile([P, PACK, J - width(FIRST)], F32, "x_later")
-        x_raw[0, MIDDLE] = x_later[:, :, : width(MIDDLE)]
-        x_raw[0, LAST] = x_later[:, :, width(MIDDLE) :]
         x_bf = {}
         xq_w = {}
         xq_s = {(a, g): tile([P, width(g)], U8, f"xq_s{a}{g}") for a in range(PASSES) for g in range(len(GROUPS))}
@@ -127,25 +141,35 @@ def tile_list_tiert_bias_kernel(
         def quantize(words, scales, src):
             nc.vector.quantize_mx(out=words.bitcast(FP8X4), scales=scales, in_=src.rearrange("p c i -> p (c i)"))
 
-        def cast_x(a, g, engine, after=None):
-            x_bf[a, g] = tile([P, width(g), PACK], BF16, f"x_bf{a}{g}", after)
-            cast(engine, x_bf[a, g][:], x_raw[a, g])
+        def cast_x(a, g, engine, after=None, parts=1):
+            w = width(g) // parts
+            for c in range(parts):
+                x_bf[a, g, c] = tile([P, w, PACK], BF16, f"x_bf{a}{g}{c}", after)
+                cast(engine, x_bf[a, g, c][:], x_raw[a, g][:, :, c * w : (c + 1) * w])
 
-        def quantize_x(a, g, after=None):
-            xq_w[a, g] = tile([P, width(g)], U32, f"xq_w{a}{g}", after)
-            quantize(xq_w[a, g][:], xq_s[a, g][:], x_bf[a, g][:])
+        def quantize_x(a, g, after=None, part=0, parts=1):
+            w = width(g) // parts
+            cols = slice(part * w, (part + 1) * w)
+            if part == 0:
+                xq_w[a, g] = tile([P, width(g)], U32, f"xq_w{a}{g}", after)
+            quantize(xq_w[a, g][:, cols], xq_s[a, g][:, cols], x_bf[a, g, part][:])
 
-        def first_tier(a, u, after=None, cast_after=None):
-            wt_bf = tile([P, PAIR, PACK], BF16, f"wt_bf{a}{u}", cast_after)
-            wq_w[a, u] = tile([P, PAIR], U32, f"wq_w{a}{u}", after)
-            cast("scalar", wt_bf[:], wt_raw[a][u])
-            quantize(wq_w[a, u][:], wq_s[a, u][:], wt_bf[:])
+        def cast_wt(a, u, parts, after=None, pad=0):
+            w = PAIR // parts
+            for c in range(parts):
+                wt_bf[a, u, c] = tile([P, w, PACK], BF16, f"wt_bf{a}{u}{c}", after, pad)
+                cast("scalar", wt_bf[a, u, c][:], wt_raw[a][u][:, :, c * w : (c + 1) * w])
 
-        def leftover(a, n):
+        def first_tier(a, u, part=0, parts=1, after=None):
+            w = PAIR // parts
+            cols = slice(part * w, (part + 1) * w)
+            if part == 0:
+                wq_w[a, u] = tile([P, PAIR], U32, f"wq_w{a}{u}", after)
+            quantize(wq_w[a, u][:, cols], wq_s[a, u][:, cols], wt_bf[a, u, part][:])
+
+        def decode(a, n):
             u, c = divmod(n, 2)
             cols = slice(c * P, (c + 1) * P)
-            if c == 0:
-                wr_bf[a, u] = tile([P, PAIR, PACK], BF16, f"wr_bf{a}{u}")
             for i in range(PACK):
                 part = slice(i * P, (i + 1) * P)
                 nc.tensor.matmul_mx(
@@ -157,12 +181,44 @@ def tile_list_tiert_bias_kernel(
                     start=True,
                     stop=True,
                 )
+            decoded[a, n] = borrowed_bank(a, n)[:]
+
+        def free_bank(a, n):
+            values = tile([P, BANK], F32, f"wq_values{a}{n}")
+            nc.scalar.activation(out=values[:], in_=decoded[a, n], func=IDENTITY)
+            decoded[a, n] = values[:]
+
+        def subtract(a, n, after=None):
+            u, c = divmod(n, 2)
+            cols = slice(c * P, (c + 1) * P)
+            if c == 0:
+                wr_bf[a, u] = tile([P, PAIR, PACK], BF16, f"wr_bf{a}{u}", after)
             nc.vector.tensor_tensor(
                 out=cols_view(wr_bf[a, u][:, cols, :]),
                 in0=rows_view(wt_raw[a][u][:, :, cols]),
-                in1=rows_view(borrowed_bank(a, n)[:].rearrange("p (i c) -> p i c", i=PACK)),
+                in1=rows_view(decoded[a, n].rearrange("p (i c) -> p i c", i=PACK)),
                 op=SUBTRACT,
             )
+
+        def subtract_on_gpsimd(a, n):
+            u, c = divmod(n, 2)
+            cols = slice(c * P, (c + 1) * P)
+            values = tile([P, P, PACK], F32, f"wq_values{a}{n}")
+            nc.scalar.activation(
+                out=values[:], in_=decoded[a, n].rearrange("p (i c) -> p c i", i=PACK), func=IDENTITY
+            )
+            if c == 0:
+                wr_bf[a, u] = tile([P, PAIR, PACK], BF16, f"wr_bf{a}{u}")
+            nc.gpsimd.tensor_tensor(
+                out=wr_bf[a, u][:, cols, :],
+                in0=wt_raw[a][u][:, :, cols].rearrange("p i c -> p c i"),
+                in1=values[:],
+                op=SUBTRACT,
+            )
+
+        def leftover(a, n, after=None):
+            decode(a, n)
+            subtract(a, n, after)
 
         def second_tier(a, u, after=None):
             wr_w[a, u] = tile([P, PAIR], U32, f"wr_w{a}{u}", after)
@@ -174,13 +230,13 @@ def tile_list_tiert_bias_kernel(
             nc.vector.tensor_copy(out=dst[:], in_=window.indirect(entries))
             return dst
 
-        def gather_scales(g, after):
+        def gather_scales(g, after=None):
             pick_s[g] = gather(tab_s[:].bitcast(U8), g, f"pick_s{g}", after)
 
         def gather_words(a, g, after=None):
             pick_w[a, g] = gather(tab_w[a][:].bitcast(U32), g, f"pick_w{a}{g}", after)
 
-        def table_passes(words, scales, a, g, tiles, first):
+        def table_passes(words, scales, a, g, tiles, first, last=False):
             for n in tiles:
                 u, c = divmod(n, 2)
                 cols = slice(c * P, (c + 1) * P)
@@ -191,17 +247,17 @@ def tile_list_tiert_bias_kernel(
                     rhs=pick_w[a, g][:].bitcast(FP8X4),
                     rhs_scale=pick_s[g][4 * a :, :],
                     start=first and opens_bank(g, n),
-                    stop=False,
+                    stop=last,
                 )
 
         def q_passes(a, g):
             table_passes(wq_w, wq_s, a, g, range(N_TILES), a == 0)
 
-        def r_passes(a, g, tiles=range(N_TILES)):
-            table_passes(wr_w, wr_s, a, g, tiles, False)
+        def r_passes(a, g, tiles=range(N_TILES), last=False):
+            table_passes(wr_w, wr_s, a, g, tiles, False, last)
 
-        def x_passes(a, g):
-            for n in range(N_TILES):
+        def x_passes(a, g, last, tiles=range(N_TILES)):
+            for n in tiles:
                 cols = slice(n * P, (n + 1) * P)
                 nc.tensor.matmul_mx(
                     out=sums(g, n),
@@ -210,11 +266,11 @@ def tile_list_tiert_bias_kernel(
                     rhs=xq_w[a, g][:].bitcast(FP8X4),
                     rhs_scale=xq_s[a, g][:],
                     start=False,
-                    stop=a == PASSES - 1 and closes_bank(g, n),
+                    stop=n in last and closes_bank(g, n),
                 )
 
-        def finish(g, engines, tiles_a_store):
-            result = tile([P, N_TILES, width(g)], F32, f"result{g}")
+        def finish(g, engines, tiles_a_store, after=None):
+            result = tile([P, N_TILES, width(g)], F32, f"result{g}", after)
             for n, engine in enumerate(engines):
                 if engine == "scalar":
                     nc.scalar.activation(out=result[:, n, :], in_=sums(g, n), func=IDENTITY, bias=bias[:, n : n + 1])
@@ -245,8 +301,9 @@ def tile_list_tiert_bias_kernel(
         load_x(0, FIRST)
         load_x(1, FIRST)
         load_words(wx_w[1], wx_words[1])
-        load_rows(x_later[:], x, 0, slice(width(FIRST), J))
+        load_x(0, MIDDLE)
         load_x(1, MIDDLE)
+        load_x(0, LAST)
         load_x(1, LAST)
 
         nc.gpsimd.memset(ones[:], 0.0)
@@ -267,14 +324,16 @@ def tile_list_tiert_bias_kernel(
         nc.vector.tensor_copy(out=unit[:], in_=ones[:, PACK - 1 : K_PASS : PACK])
 
         gather_scales(FIRST, after="eye_bf0")
+        cast_wt(0, 0, 1)
+        cast_wt(0, 1, 1)
         first_tier(0, 0, after="eye_bf1")
-        gather_scales(MIDDLE, after="wt_bf00")
+        gather_scales(MIDDLE, after="wt_bf000")
         leftover(0, 0)
         first_tier(0, 1, after="ones")
         leftover(0, 1)
         nc.tensor.transpose(sums(FIRST, N_TILES - 1)[:, :P], bias_rows[:], unit[:])
         nc.scalar.activation(out=bias[:], in_=sums(FIRST, N_TILES - 1)[:, :N_TILES], func=IDENTITY)
-        gather_words(0, FIRST, after="wt_bf01")
+        gather_words(0, FIRST, after="wt_bf010")
         second_tier(0, 0)
         leftover(0, 2)
         gather_words(0, MIDDLE, after="wr_bf00")
@@ -283,16 +342,18 @@ def tile_list_tiert_bias_kernel(
             q_passes(0, g)
             r_passes(0, g, LOW_TILES)
 
+        cast_wt(1, 0, 1)
         first_tier(1, 0)
         second_tier(0, 1)
         gather_words(1, FIRST)
-        first_tier(1, 1, cast_after="wt_bf10")
+        cast_wt(1, 1, 1, after="wt_bf100")
+        first_tier(1, 1)
         leftover(1, 0)
         leftover(1, 1)
         r_passes(0, FIRST, HIGH_TILES)
         r_passes(0, MIDDLE, HIGH_TILES)
         q_passes(1, FIRST)
-        gather_words(1, MIDDLE, after="wt_bf10")
+        gather_words(1, MIDDLE, after="wt_bf110")
         second_tier(1, 0)
         leftover(1, 2)
         leftover(1, 3)
@@ -302,33 +363,33 @@ def tile_list_tiert_bias_kernel(
         cast_x(0, FIRST, "scalar")
         quantize_x(0, FIRST, after="wr_bf10")
         second_tier(1, 1, after="x_raw00")
-        x_passes(0, FIRST)
+        x_passes(0, FIRST, ())
         r_passes(1, FIRST, HIGH_TILES)
-        r_passes(1, MIDDLE, HIGH_TILES)
-
-        gather_scales(LAST, after="x_bf00")
-        gather_words(0, LAST, after="wr_bf11")
-        q_passes(0, LAST)
-        r_passes(0, LAST)
         cast_x(1, FIRST, "scalar")
         cast_x(0, MIDDLE, "scalar")
+        gather_scales(LAST, after="x_bf000")
         quantize_x(1, FIRST)
-        x_passes(1, FIRST)
-        gather_words(1, LAST, after="x_bf10")
+        x_passes(1, FIRST, range(N_TILES))
+        r_passes(1, MIDDLE, HIGH_TILES)
+        gather_words(0, LAST, after="x_raw10")
+        gather_words(1, LAST, after="x_bf100")
+        q_passes(0, LAST)
+        r_passes(0, LAST)
         q_passes(1, LAST)
 
-        finish(FIRST, ("scalar",) * N_TILES, tiles_a_store=1)
-        cast_x(1, MIDDLE, "vector", after="tab_w1")
+        finish(FIRST, ("scalar",) * N_TILES, tiles_a_store=1, after="x_raw01")
+        cast_x(1, MIDDLE, "vector", after="tab_w0")
         quantize_x(0, MIDDLE)
         quantize_x(1, MIDDLE)
-        cast_x(0, LAST, "vector", after="x_bf01")
+        cast_x(0, LAST, "vector", after="x_bf010")
+        cast_x(1, LAST, "vector", after="x_bf110")
         quantize_x(0, LAST)
-        x_passes(0, MIDDLE)
-        x_passes(1, MIDDLE)
-        r_passes(1, LAST)
-        x_passes(0, LAST)
-        finish(MIDDLE, ("scalar",) * N_TILES, tiles_a_store=2)
-        cast_x(1, LAST, "vector")
         quantize_x(1, LAST)
-        x_passes(1, LAST)
+        x_passes(0, MIDDLE, ())
+        x_passes(1, MIDDLE, range(N_TILES))
+        r_passes(1, LAST)
+        finish(MIDDLE, ("scalar",) * N_TILES, tiles_a_store=2)
+        for tiles in (LOW_TILES, HIGH_TILES):
+            x_passes(0, LAST, (), tiles)
+            x_passes(1, LAST, tiles, tiles)
         finish(LAST, ("scalar", "scalar", "vector", "vector"), tiles_a_store=1)

@@ -65,14 +65,16 @@ def tile_list_tiert_bias_kernel(
         banks = [psum.tile([P, BANK], F32, name=f"bank{i}") for i in range(BANKS)]
 
         def sums(g, n):
+            if g == LAST:
+                return banks[(BANKS - 2 + n) % BANKS][:, : width(g)]
             bank, col = divmod(GROUPS[g].start * N_TILES + n * width(g), BANK)
             return banks[bank][:, col : col + width(g)]
 
         def opens_bank(g, n):
-            return n * width(g) % BANK == 0
+            return g == LAST or n * width(g) % BANK == 0
 
         def closes_bank(g, n):
-            return (n + 1) * width(g) % BANK == 0
+            return g == LAST or (n + 1) * width(g) % BANK == 0
 
         def borrowed_bank(a, n):
             return banks[BANKS // 2 + n] if a == 0 else banks[BANKS - 2 + n % 2]
@@ -97,10 +99,12 @@ def tile_list_tiert_bias_kernel(
         wr_w = {}
         wr_s = {(a, u): tile([P, PAIR], U8, f"wr_s{a}{u}") for a in range(PASSES) for u in range(2)}
         x_raw = {
-            (a, g): tile([P, PACK, width(g)], F32, f"x_raw{a}{g}", pad=4096 if (a, g) == (0, MIDDLE) else 0)[:]
-            for a in range(PASSES)
-            for g in range(len(GROUPS))
+            (a, g): tile([P, PACK, width(g)], F32, f"x_raw{a}{g}", pad=4096 if (a, g) == (1, MIDDLE) else 0)[:]
+            for a, g in ((0, FIRST), (1, FIRST), (1, MIDDLE), (1, LAST))
         }
+        x_later = tile([P, PACK, J - width(FIRST)], F32, "x_later")
+        x_raw[0, MIDDLE] = x_later[:, :, : width(MIDDLE)]
+        x_raw[0, LAST] = x_later[:, :, width(MIDDLE) :]
         x_bf = {}
         xq_w = {}
         xq_s = {(a, g): tile([P, width(g)], U8, f"xq_s{a}{g}") for a in range(PASSES) for g in range(len(GROUPS))}
@@ -250,8 +254,8 @@ def tile_list_tiert_bias_kernel(
                     stop=last,
                 )
 
-        def q_passes(a, g):
-            table_passes(wq_w, wq_s, a, g, range(N_TILES), a == 0)
+        def q_passes(a, g, tiles=range(N_TILES)):
+            table_passes(wq_w, wq_s, a, g, tiles, a == 0)
 
         def r_passes(a, g, tiles=range(N_TILES), last=False):
             table_passes(wr_w, wr_s, a, g, tiles, False, last)
@@ -301,9 +305,8 @@ def tile_list_tiert_bias_kernel(
         load_x(0, FIRST)
         load_x(1, FIRST)
         load_words(wx_w[1], wx_words[1])
-        load_x(0, MIDDLE)
         load_x(1, MIDDLE)
-        load_x(0, LAST)
+        load_rows(x_later[:], x, 0, slice(width(FIRST), J))
         load_x(1, LAST)
 
         nc.gpsimd.memset(ones[:], 0.0)
@@ -365,31 +368,35 @@ def tile_list_tiert_bias_kernel(
         second_tier(1, 1, after="x_raw00")
         x_passes(0, FIRST, ())
         r_passes(1, FIRST, HIGH_TILES)
-        cast_x(1, FIRST, "scalar")
-        cast_x(0, MIDDLE, "scalar")
+        cast_x(1, FIRST, "scalar", parts=2)
+        cast_x(1, MIDDLE, "scalar")
         gather_scales(LAST, after="x_bf000")
-        quantize_x(1, FIRST)
+        quantize_x(1, FIRST, part=0, parts=2)
+        quantize_x(1, FIRST, part=1, parts=2)
         x_passes(1, FIRST, range(N_TILES))
         r_passes(1, MIDDLE, HIGH_TILES)
         gather_words(0, LAST, after="x_raw10")
-        gather_words(1, LAST, after="x_bf100")
-        q_passes(0, LAST)
-        r_passes(0, LAST)
-        q_passes(1, LAST)
+        gather_words(1, LAST, after="x_bf101")
+        q_passes(0, LAST, LOW_TILES)
+        r_passes(0, LAST, LOW_TILES)
+        q_passes(1, LAST, LOW_TILES)
 
-        finish(FIRST, ("scalar",) * N_TILES, tiles_a_store=1, after="x_raw01")
-        cast_x(1, MIDDLE, "vector", after="tab_w0")
-        quantize_x(0, MIDDLE)
+        finish(FIRST, ("scalar",) * N_TILES, tiles_a_store=1, after="x_raw11")
+        cast_x(0, MIDDLE, "vector", after="tab_w0")
         quantize_x(1, MIDDLE)
-        cast_x(0, LAST, "vector", after="x_bf010")
-        cast_x(1, LAST, "vector", after="x_bf110")
+        quantize_x(0, MIDDLE)
+        cast_x(0, LAST, "vector", after="x_bf110")
+        cast_x(1, LAST, "vector", after="x_bf010")
         quantize_x(0, LAST)
         quantize_x(1, LAST)
-        x_passes(0, MIDDLE, ())
-        x_passes(1, MIDDLE, range(N_TILES))
+        x_passes(1, MIDDLE, ())
+        x_passes(0, MIDDLE, range(N_TILES))
+        q_passes(0, LAST, HIGH_TILES)
+        r_passes(0, LAST, HIGH_TILES)
+        q_passes(1, LAST, HIGH_TILES)
         r_passes(1, LAST)
         finish(MIDDLE, ("scalar",) * N_TILES, tiles_a_store=2)
-        for tiles in (LOW_TILES, HIGH_TILES):
-            x_passes(0, LAST, (), tiles)
-            x_passes(1, LAST, tiles, tiles)
-        finish(LAST, ("scalar", "scalar", "vector", "vector"), tiles_a_store=1)
+        for n in range(N_TILES):
+            x_passes(0, LAST, (), (n,))
+            x_passes(1, LAST, (n,), (n,))
+        finish(LAST, ("scalar", "vector", "scalar", "vector"), tiles_a_store=1)

@@ -16,8 +16,6 @@ IDENTITY = mybir.ActivationFunctionType.Identity
 SUBTRACT = mybir.AluOpType.subtract
 ADD = mybir.AluOpType.add
 
-ELEMENT_BYTES = ((F32, 4), (I32, 4), (U32, 4), (BF16, 2), (U8, 1))
-ALIGN = 64
 P = 128
 PACK = 4
 K_PASS = P * PACK
@@ -33,6 +31,8 @@ RUN = 4
 
 GROUPS = (slice(0, 512), slice(512, 768), slice(768, 1024))
 FIRST, MIDDLE, LAST = range(len(GROUPS))
+PIECE = 256
+PIECES = ((slice(0, PIECE), slice(PIECE, 2 * PIECE)), (slice(0, PIECE),), (slice(0, PIECE),))
 
 
 def tile_list_tiert_bias_kernel(
@@ -41,22 +41,10 @@ def tile_list_tiert_bias_kernel(
     nc = tc.nc
     with ExitStack() as ctx:
         sb = ctx.enter_context(tc.tile_pool(name="sb", bufs=1))
-        arena = ctx.enter_context(tc.tile_pool(name="arena", bufs=1))
         psum = ctx.enter_context(tc.psum_pool(name="psum", bufs=1))
-        place = {"end": 0}
 
-        def tile(shape, dtype, name, after=None, pad=0):
-            if after is None:
-                place[name] = place["end"] + pad
-                size = [n for t, n in ELEMENT_BYTES if t == dtype][0]
-                for n in shape[1:]:
-                    size = size * n
-                place["end"] = place["end"] + 2 * pad + -(-size // ALIGN) * ALIGN
-            elif isinstance(after, tuple):
-                place[name] = place[after[0]] + after[1]
-            else:
-                place[name] = place[after]
-            return arena.tile(shape, dtype, name=name, offset=place[name], align_bytes=ALIGN)
+        def tile(shape, dtype, name, after=None):
+            return sb.tile(shape, dtype, name=name, tag=after or name, align_bytes=64)
 
         def width(g):
             return GROUPS[g].stop - GROUPS[g].start
@@ -65,16 +53,16 @@ def tile_list_tiert_bias_kernel(
         banks = [psum.tile([P, BANK], F32, name=f"bank{i}") for i in range(BANKS)]
 
         def sums(g, n):
-            if g == LAST:
-                return banks[(BANKS - 2 + n) % BANKS][:, : width(g)]
-            bank, col = divmod(GROUPS[g].start * N_TILES + n * width(g), BANK)
-            return banks[bank][:, col : col + width(g)]
+            if g == MIDDLE:
+                return banks[N_TILES + n // 2][:, n % 2 * width(g) : (n % 2 + 1) * width(g)]
+            first_bank = 0 if g == FIRST else BANKS - 2
+            return banks[(first_bank + n) % BANKS][:, : width(g)]
 
         def opens_bank(g, n):
-            return g == LAST or n * width(g) % BANK == 0
+            return g != MIDDLE or n % 2 == 0
 
         def closes_bank(g, n):
-            return g == LAST or (n + 1) * width(g) % BANK == 0
+            return g != MIDDLE or n % 2 == 1
 
         def borrowed_bank(a, n):
             return banks[BANKS // 2 + n] if a == 0 else banks[BANKS - 2 + n % 2]
@@ -94,12 +82,11 @@ def tile_list_tiert_bias_kernel(
         wt_bf = {}
         wq_w = {}
         wq_s = {(a, u): tile([P, PAIR], U8, f"wq_s{a}{u}") for a in range(PASSES) for u in range(2)}
-        decoded = {}
         wr_bf = {}
         wr_w = {}
         wr_s = {(a, u): tile([P, PAIR], U8, f"wr_s{a}{u}") for a in range(PASSES) for u in range(2)}
         x_raw = {
-            (a, g): tile([P, PACK, width(g)], F32, f"x_raw{a}{g}", pad=4096 if (a, g) == (1, MIDDLE) else 0)[:]
+            (a, g): tile([P, PACK, width(g)], F32, f"x_raw{a}{g}")[:]
             for a, g in ((0, FIRST), (1, FIRST), (1, MIDDLE), (1, LAST))
         }
         x_later = tile([P, PACK, J - width(FIRST)], F32, "x_later")
@@ -145,35 +132,30 @@ def tile_list_tiert_bias_kernel(
         def quantize(words, scales, src):
             nc.vector.quantize_mx(out=words.bitcast(FP8X4), scales=scales, in_=src.rearrange("p c i -> p (c i)"))
 
-        def cast_x(a, g, engine, after=None, parts=1):
-            w = width(g) // parts
-            for c in range(parts):
-                x_bf[a, g, c] = tile([P, w, PACK], BF16, f"x_bf{a}{g}{c}", after)
-                cast(engine, x_bf[a, g, c][:], x_raw[a, g][:, :, c * w : (c + 1) * w])
+        def cast_x(a, g, engine, after=None):
+            for c, tokens in enumerate(PIECES[g]):
+                x_bf[a, g, c] = tile([P, PIECE, PACK], BF16, f"x_bf{a}{g}{c}", after)
+                cast(engine, x_bf[a, g, c][:], x_raw[a, g][:, :, tokens])
 
-        def quantize_x(a, g, after=None, part=0, parts=1):
-            w = width(g) // parts
-            cols = slice(part * w, (part + 1) * w)
-            if part == 0:
+        def quantize_x(a, g, c=0, after=None):
+            if c == 0:
                 xq_w[a, g] = tile([P, width(g)], U32, f"xq_w{a}{g}", after)
-            quantize(xq_w[a, g][:, cols], xq_s[a, g][:, cols], x_bf[a, g, part][:])
+            tokens = PIECES[g][c]
+            quantize(xq_w[a, g][:, tokens], xq_s[a, g][:, tokens], x_bf[a, g, c][:])
 
-        def cast_wt(a, u, parts, after=None, pad=0):
-            w = PAIR // parts
-            for c in range(parts):
-                wt_bf[a, u, c] = tile([P, w, PACK], BF16, f"wt_bf{a}{u}{c}", after, pad)
-                cast("scalar", wt_bf[a, u, c][:], wt_raw[a][u][:, :, c * w : (c + 1) * w])
+        def cast_wt(a, u, after=None):
+            wt_bf[a, u] = tile([P, PAIR, PACK], BF16, f"wt_bf{a}{u}", after)
+            cast("scalar", wt_bf[a, u][:], wt_raw[a][u])
 
-        def first_tier(a, u, part=0, parts=1, after=None):
-            w = PAIR // parts
-            cols = slice(part * w, (part + 1) * w)
-            if part == 0:
-                wq_w[a, u] = tile([P, PAIR], U32, f"wq_w{a}{u}", after)
-            quantize(wq_w[a, u][:, cols], wq_s[a, u][:, cols], wt_bf[a, u, part][:])
+        def first_tier(a, u, after=None):
+            wq_w[a, u] = tile([P, PAIR], U32, f"wq_w{a}{u}", after)
+            quantize(wq_w[a, u][:], wq_s[a, u][:], wt_bf[a, u][:])
 
-        def decode(a, n):
+        def leftover(a, n):
             u, c = divmod(n, 2)
             cols = slice(c * P, (c + 1) * P)
+            if c == 0:
+                wr_bf[a, u] = tile([P, PAIR, PACK], BF16, f"wr_bf{a}{u}")
             for i in range(PACK):
                 part = slice(i * P, (i + 1) * P)
                 nc.tensor.matmul_mx(
@@ -185,44 +167,12 @@ def tile_list_tiert_bias_kernel(
                     start=True,
                     stop=True,
                 )
-            decoded[a, n] = borrowed_bank(a, n)[:]
-
-        def free_bank(a, n):
-            values = tile([P, BANK], F32, f"wq_values{a}{n}")
-            nc.scalar.activation(out=values[:], in_=decoded[a, n], func=IDENTITY)
-            decoded[a, n] = values[:]
-
-        def subtract(a, n, after=None):
-            u, c = divmod(n, 2)
-            cols = slice(c * P, (c + 1) * P)
-            if c == 0:
-                wr_bf[a, u] = tile([P, PAIR, PACK], BF16, f"wr_bf{a}{u}", after)
             nc.vector.tensor_tensor(
                 out=cols_view(wr_bf[a, u][:, cols, :]),
                 in0=rows_view(wt_raw[a][u][:, :, cols]),
-                in1=rows_view(decoded[a, n].rearrange("p (i c) -> p i c", i=PACK)),
+                in1=rows_view(borrowed_bank(a, n)[:].rearrange("p (i c) -> p i c", i=PACK)),
                 op=SUBTRACT,
             )
-
-        def subtract_on_gpsimd(a, n):
-            u, c = divmod(n, 2)
-            cols = slice(c * P, (c + 1) * P)
-            values = tile([P, P, PACK], F32, f"wq_values{a}{n}")
-            nc.scalar.activation(
-                out=values[:], in_=decoded[a, n].rearrange("p (i c) -> p c i", i=PACK), func=IDENTITY
-            )
-            if c == 0:
-                wr_bf[a, u] = tile([P, PAIR, PACK], BF16, f"wr_bf{a}{u}")
-            nc.gpsimd.tensor_tensor(
-                out=wr_bf[a, u][:, cols, :],
-                in0=wt_raw[a][u][:, :, cols].rearrange("p i c -> p c i"),
-                in1=values[:],
-                op=SUBTRACT,
-            )
-
-        def leftover(a, n, after=None):
-            decode(a, n)
-            subtract(a, n, after)
 
         def second_tier(a, u, after=None):
             wr_w[a, u] = tile([P, PAIR], U32, f"wr_w{a}{u}", after)
@@ -234,13 +184,13 @@ def tile_list_tiert_bias_kernel(
             nc.vector.tensor_copy(out=dst[:], in_=window.indirect(entries))
             return dst
 
-        def gather_scales(g, after=None):
+        def gather_scales(g, after):
             pick_s[g] = gather(tab_s[:].bitcast(U8), g, f"pick_s{g}", after)
 
         def gather_words(a, g, after=None):
             pick_w[a, g] = gather(tab_w[a][:].bitcast(U32), g, f"pick_w{a}{g}", after)
 
-        def table_passes(words, scales, a, g, tiles, first, last=False):
+        def table_passes(words, scales, a, g, tiles, first):
             for n in tiles:
                 u, c = divmod(n, 2)
                 cols = slice(c * P, (c + 1) * P)
@@ -251,26 +201,26 @@ def tile_list_tiert_bias_kernel(
                     rhs=pick_w[a, g][:].bitcast(FP8X4),
                     rhs_scale=pick_s[g][4 * a :, :],
                     start=first and opens_bank(g, n),
-                    stop=last,
+                    stop=False,
                 )
 
         def q_passes(a, g, tiles=range(N_TILES)):
             table_passes(wq_w, wq_s, a, g, tiles, a == 0)
 
-        def r_passes(a, g, tiles=range(N_TILES), last=False):
-            table_passes(wr_w, wr_s, a, g, tiles, False, last)
+        def r_passes(a, g, tiles=range(N_TILES)):
+            table_passes(wr_w, wr_s, a, g, tiles, False)
 
-        def x_passes(a, g, last, tiles=range(N_TILES)):
+        def x_passes(a, g, tiles=range(N_TILES), tokens=slice(None), last=False):
             for n in tiles:
                 cols = slice(n * P, (n + 1) * P)
                 nc.tensor.matmul_mx(
-                    out=sums(g, n),
+                    out=sums(g, n)[:, tokens],
                     lhsT=wx_w[a][:, cols].bitcast(FP8X4),
                     lhsT_scale=wx_s[4 * a :, :].bitcast(U8)[:, cols],
-                    rhs=xq_w[a, g][:].bitcast(FP8X4),
-                    rhs_scale=xq_s[a, g][:],
+                    rhs=xq_w[a, g][:, tokens].bitcast(FP8X4),
+                    rhs_scale=xq_s[a, g][:, tokens],
                     start=False,
-                    stop=n in last and closes_bank(g, n),
+                    stop=last and closes_bank(g, n),
                 )
 
         def finish(g, engines, tiles_a_store, after=None):
@@ -327,16 +277,16 @@ def tile_list_tiert_bias_kernel(
         nc.vector.tensor_copy(out=unit[:], in_=ones[:, PACK - 1 : K_PASS : PACK])
 
         gather_scales(FIRST, after="eye_bf0")
-        cast_wt(0, 0, 1)
-        cast_wt(0, 1, 1)
+        cast_wt(0, 0)
+        cast_wt(0, 1)
         first_tier(0, 0, after="eye_bf1")
-        gather_scales(MIDDLE, after="wt_bf000")
+        gather_scales(MIDDLE, after="wt_bf00")
         leftover(0, 0)
         first_tier(0, 1, after="ones")
         leftover(0, 1)
         nc.tensor.transpose(sums(FIRST, N_TILES - 1)[:, :P], bias_rows[:], unit[:])
         nc.scalar.activation(out=bias[:], in_=sums(FIRST, N_TILES - 1)[:, :N_TILES], func=IDENTITY)
-        gather_words(0, FIRST, after="wt_bf010")
+        gather_words(0, FIRST, after="wt_bf01")
         second_tier(0, 0)
         leftover(0, 2)
         gather_words(0, MIDDLE, after="wr_bf00")
@@ -345,35 +295,38 @@ def tile_list_tiert_bias_kernel(
             q_passes(0, g)
             r_passes(0, g, LOW_TILES)
 
-        cast_wt(1, 0, 1)
+        cast_wt(1, 0)
         first_tier(1, 0)
         second_tier(0, 1)
         gather_words(1, FIRST)
-        cast_wt(1, 1, 1, after="wt_bf100")
+        cast_wt(1, 1, after="wt_bf10")
         first_tier(1, 1)
         leftover(1, 0)
         leftover(1, 1)
         r_passes(0, FIRST, HIGH_TILES)
         r_passes(0, MIDDLE, HIGH_TILES)
         q_passes(1, FIRST)
-        gather_words(1, MIDDLE, after="wt_bf110")
+        gather_words(1, MIDDLE, after="wt_bf10")
         second_tier(1, 0)
         leftover(1, 2)
+        cast_x(0, FIRST, "scalar")
+        quantize_x(0, FIRST, 0, after="wr_bf10")
         leftover(1, 3)
         r_passes(1, FIRST, LOW_TILES)
         q_passes(1, MIDDLE)
         r_passes(1, MIDDLE, LOW_TILES)
-        cast_x(0, FIRST, "scalar")
-        quantize_x(0, FIRST, after="wr_bf10")
+        x_passes(0, FIRST, tokens=PIECES[FIRST][0])
+        quantize_x(0, FIRST, 1)
         second_tier(1, 1, after="x_raw00")
-        x_passes(0, FIRST, ())
+        x_passes(0, FIRST, tokens=PIECES[FIRST][1])
         r_passes(1, FIRST, HIGH_TILES)
-        cast_x(1, FIRST, "scalar", parts=2)
+
+        cast_x(1, FIRST, "scalar")
         cast_x(1, MIDDLE, "scalar")
-        gather_scales(LAST, after="x_bf000")
-        quantize_x(1, FIRST, part=0, parts=2)
-        quantize_x(1, FIRST, part=1, parts=2)
-        x_passes(1, FIRST, range(N_TILES))
+        gather_scales(LAST, after="x_bf001")
+        quantize_x(1, FIRST, 0)
+        quantize_x(1, FIRST, 1)
+        x_passes(1, FIRST, last=True)
         r_passes(1, MIDDLE, HIGH_TILES)
         gather_words(0, LAST, after="x_raw10")
         gather_words(1, LAST, after="x_bf101")
@@ -389,14 +342,14 @@ def tile_list_tiert_bias_kernel(
         cast_x(1, LAST, "vector", after="x_bf010")
         quantize_x(0, LAST)
         quantize_x(1, LAST)
-        x_passes(1, MIDDLE, ())
-        x_passes(0, MIDDLE, range(N_TILES))
+        x_passes(1, MIDDLE)
+        x_passes(0, MIDDLE, last=True)
         q_passes(0, LAST, HIGH_TILES)
         r_passes(0, LAST, HIGH_TILES)
         q_passes(1, LAST, HIGH_TILES)
         r_passes(1, LAST)
         finish(MIDDLE, ("scalar",) * N_TILES, tiles_a_store=2)
         for n in range(N_TILES):
-            x_passes(0, LAST, (), (n,))
-            x_passes(1, LAST, (n,), (n,))
-        finish(LAST, ("scalar", "vector", "scalar", "vector"), tiles_a_store=1)
+            x_passes(0, LAST, (n,))
+            x_passes(1, LAST, (n,), last=True)
+        finish(LAST, ("scalar", "vector") * 2, tiles_a_store=1)

@@ -16,6 +16,7 @@ IDENTITY = mybir.ActivationFunctionType.Identity
 SUBTRACT = mybir.AluOpType.subtract
 ADD = mybir.AluOpType.add
 
+ALIGN = 256
 P = 128
 PACK = 4
 K_PASS = P * PACK
@@ -44,7 +45,7 @@ def tile_list_tiert_bias_kernel(
         psum = ctx.enter_context(tc.psum_pool(name="psum", bufs=1))
 
         def tile(shape, dtype, name, after=None):
-            return sb.tile(shape, dtype, name=name, tag=after or name, align_bytes=64)
+            return sb.tile(shape, dtype, name=name, tag=after or name, align_bytes=ALIGN)
 
         def width(g):
             return GROUPS[g].stop - GROUPS[g].start

from contextlib import ExitStack

import concourse.mybir as mybir

K, L, N, T, J = 1024, 1024, 512, 2048, 1024
FLOPS = 3758096384

F32 = mybir.dt.float32
BF16 = mybir.dt.bfloat16
I32 = mybir.dt.int32
U32 = mybir.dt.uint32
U16 = mybir.dt.uint16
U8 = mybir.dt.uint8
FP8X4 = mybir.dt.float8_e4m3fn_x4
IDENTITY = mybir.ActivationFunctionType.Identity
SUBTRACT = mybir.AluOpType.subtract
ADD = mybir.AluOpType.add

ALIGN = 256
P = 128
PACK = 4
K_PASS = P * PACK
PASSES = K // K_PASS
N_TILES = N // P
PAIR = 2 * P
LOW_TILES, HIGH_TILES = (0, 1), (2, 3)
BANK = 512
BANKS = 8
QUADRANT = 32
LIST_ROWS = 16
RUN = 4

GROUPS = (slice(0, 512), slice(512, 768), slice(768, 1024))
FIRST, MIDDLE, LAST = range(len(GROUPS))
PIECE = 256
PIECES = ((slice(0, PIECE), slice(PIECE, 2 * PIECE)), (slice(0, PIECE),), (slice(0, PIECE),))


def tile_list_tiert_bias_kernel(
    tc, tab_words, tab_scales, wt, x, wx_words, wx_scales, b, offs, out
):
    nc = tc.nc
    with ExitStack() as ctx:
        sb = ctx.enter_context(tc.tile_pool(name="sb", bufs=1))
        psum = ctx.enter_context(tc.psum_pool(name="psum", bufs=1))

        def tile(shape, dtype, name, after=None):
            return sb.tile(shape, dtype, name=name, tag=after or name, align_bytes=ALIGN)

        def width(g):
            return GROUPS[g].stop - GROUPS[g].start

        offsets = sb.tile([P, J // LIST_ROWS], U16, name="offsets")
        banks = [psum.tile([P, BANK], F32, name=f"bank{i}") for i in range(BANKS)]

        def sums(g, n):
            if g == MIDDLE:
                return banks[N_TILES + n // 2][:, n % 2 * width(g) : (n % 2 + 1) * width(g)]
            first_bank = 0 if g == FIRST else BANKS - 2
            return banks[(first_bank + n) % BANKS][:, : width(g)]

        def opens_bank(g, n):
            return g != MIDDLE or n % 2 == 0

        def closes_bank(g, n):
            return g != MIDDLE or n % 2 == 1

        def borrowed_bank(a, n):
            return banks[BANKS // 2 + n] if a == 0 else banks[BANKS - 2 + n % 2]

        tab_s = tile([P, T // 4], I32, "tab_s")
        tab_w = [tile([P, T], I32, f"tab_w{a}") for a in range(PASSES)]
        pick_s = {}
        pick_w = {}
        wx_s = tile([P, N // 4], I32, "wx_s")
        wx_w = [tile([P, N], I32, f"wx_w{a}") for a in range(PASSES)]
        bias = tile([P, N_TILES], F32, "bias")
        bias_rows = tile([P, P], F32, "bias_rows")
        unit = tile([P, P], F32, "unit")
        wt_first = [tile([P, PACK, PAIR], F32, f"wt_raw0{u}") for u in range(2)]
        wt_second = tile([P, PACK, N], F32, "wt_raw1")
        wt_raw = [[t[:] for t in wt_first], [wt_second[:, :, u * PAIR : (u + 1) * PAIR] for u in range(2)]]
        wt_bf = {}
        wq_w = {}
        wq_s = {(a, u): tile([P, PAIR], U8, f"wq_s{a}{u}") for a in range(PASSES) for u in range(2)}
        wr_bf = {}
        wr_w = {}
        wr_s = {(a, u): tile([P, PAIR], U8, f"wr_s{a}{u}") for a in range(PASSES) for u in range(2)}
        x_raw = {
            (a, g): tile([P, PACK, width(g)], F32, f"x_raw{a}{g}")[:]
            for a, g in ((0, FIRST), (1, FIRST), (1, MIDDLE), (1, LAST))
        }
        x_later = tile([P, PACK, J - width(FIRST)], F32, "x_later")
        x_raw[0, MIDDLE] = x_later[:, :, : width(MIDDLE)]
        x_raw[0, LAST] = x_later[:, :, width(MIDDLE) :]
        x_bf = {}
        xq_w = {}
        xq_s = {(a, g): tile([P, width(g)], U8, f"xq_s{a}{g}") for a in range(PASSES) for g in range(len(GROUPS))}
        ones = tile([P, K_PASS + PACK], BF16, "ones")
        eye_bf = [tile([P, 2, K_PASS], BF16, f"eye_bf{v}") for v in range(2)]
        eye_w = tile([P, PACK * P], U32, "eye_w")
        eye_s = tile([P, PACK * P], U8, "eye_s")

        def load_scales(dst, src):
            for q in range(P // QUADRANT):
                nc.sync.dma_start(
                    out=dst[QUADRANT * q : QUADRANT * q + 4 * PASSES, :],
                    in_=src[:, 4 * q : 4 * q + 4, :].bitcast(I32),
                )

        def load_rows(dst, src, a, cols):
            rows = src[a * K_PASS : (a + 1) * K_PASS, cols]
            nc.sync.dma_start(out=dst, in_=rows.rearrange("(p i) c -> p i c", i=PACK))

        def load_x(a, g):
            load_rows(x_raw[a, g], x, a, GROUPS[g])

        def load_words(dst, src):
            nc.sync.dma_start(out=dst[:], in_=src.rearrange("p t i -> p (t i)").bitcast(I32))

        def rows_view(ap):
            return ap.rearrange("p i (c r) -> p c i r", r=RUN)

        def cols_view(ap):
            return ap.rearrange("p (c r) i -> p c i r", r=RUN)

        def cast(engine, dst, src):
            if engine == "scalar":
                nc.scalar.activation(out=cols_view(dst), in_=rows_view(src), func=IDENTITY)
            else:
                nc.vector.tensor_copy(out=cols_view(dst), in_=rows_view(src))

        def quantize(words, scales, src):
            nc.vector.quantize_mx(out=words.bitcast(FP8X4), scales=scales, in_=src.rearrange("p c i -> p (c i)"))

        def cast_x(a, g, engine, after=None):
            for c, tokens in enumerate(PIECES[g]):
                x_bf[a, g, c] = tile([P, PIECE, PACK], BF16, f"x_bf{a}{g}{c}", after)
                cast(engine, x_bf[a, g, c][:], x_raw[a, g][:, :, tokens])

        def quantize_x(a, g, c=0, after=None):
            if c == 0:
                xq_w[a, g] = tile([P, width(g)], U32, f"xq_w{a}{g}", after)
            tokens = PIECES[g][c]
            quantize(xq_w[a, g][:, tokens], xq_s[a, g][:, tokens], x_bf[a, g, c][:])

        def cast_wt(a, u, after=None):
            wt_bf[a, u] = tile([P, PAIR, PACK], BF16, f"wt_bf{a}{u}", after)
            cast("scalar", wt_bf[a, u][:], wt_raw[a][u])

        def first_tier(a, u, after=None):
            wq_w[a, u] = tile([P, PAIR], U32, f"wq_w{a}{u}", after)
            quantize(wq_w[a, u][:], wq_s[a, u][:], wt_bf[a, u][:])

        def leftover(a, n):
            u, c = divmod(n, 2)
            cols = slice(c * P, (c + 1) * P)
            if c == 0:
                wr_bf[a, u] = tile([P, PAIR, PACK], BF16, f"wr_bf{a}{u}")
            for i in range(PACK):
                part = slice(i * P, (i + 1) * P)
                nc.tensor.matmul_mx(
                    out=borrowed_bank(a, n)[:, part],
                    lhsT=eye_w[:, part].bitcast(FP8X4),
                    lhsT_scale=eye_s[:, part],
                    rhs=wq_w[a, u][:, cols].bitcast(FP8X4),
                    rhs_scale=wq_s[a, u][:, cols],
                    start=True,
                    stop=True,
                )
            nc.vector.tensor_tensor(
                out=cols_view(wr_bf[a, u][:, cols, :]),
                in0=rows_view(wt_raw[a][u][:, :, cols]),
                in1=rows_view(borrowed_bank(a, n)[:].rearrange("p (i c) -> p i c", i=PACK)),
                op=SUBTRACT,
            )

        def second_tier(a, u, after=None):
            wr_w[a, u] = tile([P, PAIR], U32, f"wr_w{a}{u}", after)
            quantize(wr_w[a, u][:], wr_s[a, u][:], wr_bf[a, u][:])

        def gather(window, g, name, after):
            dst = tile([P, width(g)], window.dtype, name, after)
            entries = offsets[:, GROUPS[g].start // LIST_ROWS : GROUPS[g].stop // LIST_ROWS]
            nc.vector.tensor_copy(out=dst[:], in_=window.indirect(entries))
            return dst

        def gather_scales(g, after):
            pick_s[g] = gather(tab_s[:].bitcast(U8), g, f"pick_s{g}", after)

        def gather_words(a, g, after=None):
            pick_w[a, g] = gather(tab_w[a][:].bitcast(U32), g, f"pick_w{a}{g}", after)

        def table_passes(words, scales, a, g, tiles, first):
            for n in tiles:
                u, c = divmod(n, 2)
                cols = slice(c * P, (c + 1) * P)
                nc.tensor.matmul_mx(
                    out=sums(g, n),
                    lhsT=words[a, u][:, cols].bitcast(FP8X4),
                    lhsT_scale=scales[a, u][:, cols],
                    rhs=pick_w[a, g][:].bitcast(FP8X4),
                    rhs_scale=pick_s[g][4 * a :, :],
                    start=first and opens_bank(g, n),
                    stop=False,
                )

        def q_passes(a, g, tiles=range(N_TILES)):
            table_passes(wq_w, wq_s, a, g, tiles, a == 0)

        def r_passes(a, g, tiles=range(N_TILES)):
            table_passes(wr_w, wr_s, a, g, tiles, False)

        def x_passes(a, g, tiles=range(N_TILES), tokens=slice(None), last=False):
            for n in tiles:
                cols = slice(n * P, (n + 1) * P)
                nc.tensor.matmul_mx(
                    out=sums(g, n)[:, tokens],
                    lhsT=wx_w[a][:, cols].bitcast(FP8X4),
                    lhsT_scale=wx_s[4 * a :, :].bitcast(U8)[:, cols],
                    rhs=xq_w[a, g][:, tokens].bitcast(FP8X4),
                    rhs_scale=xq_s[a, g][:, tokens],
                    start=False,
                    stop=last and closes_bank(g, n),
                )

        def finish(g, engines, tiles_a_store, after=None):
            result = tile([P, N_TILES, width(g)], F32, f"result{g}", after)
            for n, engine in enumerate(engines):
                if engine == "scalar":
                    nc.scalar.activation(out=result[:, n, :], in_=sums(g, n), func=IDENTITY, bias=bias[:, n : n + 1])
                else:
                    nc.vector.tensor_scalar(
                        out=result[:, n, :], in0=sums(g, n), scalar1=bias[:, n : n + 1], scalar2=None, op0=ADD
                    )
                if (n + 1) % tiles_a_store == 0:
                    lo = n + 1 - tiles_a_store
                    nc.sync.dma_start(
                        out=out[lo * P : (n + 1) * P, GROUPS[g]].rearrange("(n p) c -> p n c", p=P),
                        in_=result[:, lo : n + 1, :],
                    )

        nc.vector.memset(tab_s[:], 0)
        nc.sync.dma_start(offsets[:], offs)
        load_scales(tab_s, tab_scales)
        load_rows(wt_raw[0][0], wt, 0, slice(0, PAIR))
        nc.vector.memset(bias_rows[:], 0.0)
        nc.sync.dma_start(out=bias_rows[:N_TILES, :], in_=b.rearrange("(n p) -> n p", p=P))
        load_rows(wt_raw[0][1], wt, 0, slice(PAIR, N))
        load_words(tab_w[0], tab_words[0])
        load_rows(wt_second[:], wt, 1, slice(0, N))
        load_words(tab_w[1], tab_words[1])
        nc.vector.memset(wx_s[:], 0)
        load_scales(wx_s, wx_scales)
        load_words(wx_w[0], wx_words[0])
        load_x(0, FIRST)
        load_x(1, FIRST)
        load_words(wx_w[1], wx_words[1])
        load_x(1, MIDDLE)
        load_rows(x_later[:], x, 0, slice(width(FIRST), J))
        load_x(1, LAST)

        nc.gpsimd.memset(ones[:], 0.0)
        nc.gpsimd.affine_select(
            out=ones[:],
            in_=ones[:],
            compare_op=mybir.AluOpType.not_equal,
            fill=1.0,
            base=PACK - 1,
            pattern=[[-1, K_PASS + PACK]],
            channel_multiplier=PACK,
        )
        for i in range(PACK):
            nc.vector.tensor_copy(out=eye_bf[i // 2][:, i % 2, :], in_=ones[:, PACK - 1 - i : PACK - 1 - i + K_PASS])
        for v in range(2):
            cols = slice(2 * v * P, 2 * (v + 1) * P)
            quantize(eye_w[:, cols], eye_s[:, cols], eye_bf[v][:])
        nc.vector.tensor_copy(out=unit[:], in_=ones[:, PACK - 1 : K_PASS : PACK])

        gather_scales(FIRST, after="eye_bf0")
        cast_wt(0, 0)
        cast_wt(0, 1)
        first_tier(0, 0, after="eye_bf1")
        gather_scales(MIDDLE, after="wt_bf00")
        leftover(0, 0)
        first_tier(0, 1, after="ones")
        leftover(0, 1)
        nc.tensor.transpose(sums(FIRST, N_TILES - 1)[:, :P], bias_rows[:], unit[:])
        nc.scalar.activation(out=bias[:], in_=sums(FIRST, N_TILES - 1)[:, :N_TILES], func=IDENTITY)
        gather_words(0, FIRST, after="wt_bf01")
        second_tier(0, 0)
        leftover(0, 2)
        gather_words(0, MIDDLE, after="wr_bf00")
        leftover(0, 3)
        for g in (FIRST, MIDDLE):
            q_passes(0, g)
            r_passes(0, g, LOW_TILES)

        cast_wt(1, 0)
        first_tier(1, 0)
        second_tier(0, 1)
        gather_words(1, FIRST)
        cast_wt(1, 1, after="wt_bf10")
        first_tier(1, 1)
        leftover(1, 0)
        leftover(1, 1)
        r_passes(0, FIRST, HIGH_TILES)
        r_passes(0, MIDDLE, HIGH_TILES)
        q_passes(1, FIRST)
        gather_words(1, MIDDLE, after="wt_bf10")
        second_tier(1, 0)
        leftover(1, 2)
        cast_x(0, FIRST, "scalar")
        quantize_x(0, FIRST, 0, after="wr_bf10")
        leftover(1, 3)
        r_passes(1, FIRST, LOW_TILES)
        q_passes(1, MIDDLE)
        r_passes(1, MIDDLE, LOW_TILES)
        x_passes(0, FIRST, tokens=PIECES[FIRST][0])
        quantize_x(0, FIRST, 1)
        second_tier(1, 1, after="x_raw00")
        x_passes(0, FIRST, tokens=PIECES[FIRST][1])
        r_passes(1, FIRST, HIGH_TILES)

        cast_x(1, FIRST, "scalar")
        cast_x(1, MIDDLE, "scalar")
        gather_scales(LAST, after="x_bf001")
        quantize_x(1, FIRST, 0)
        quantize_x(1, FIRST, 1)
        x_passes(1, FIRST, last=True)
        r_passes(1, MIDDLE, HIGH_TILES)
        gather_words(0, LAST, after="x_raw10")
        gather_words(1, LAST, after="x_bf101")
        q_passes(0, LAST, LOW_TILES)
        r_passes(0, LAST, LOW_TILES)
        q_passes(1, LAST, LOW_TILES)

        finish(FIRST, ("scalar",) * N_TILES, tiles_a_store=1, after="x_raw11")
        cast_x(0, MIDDLE, "vector", after="tab_w0")
        quantize_x(1, MIDDLE)
        quantize_x(0, MIDDLE)
        cast_x(0, LAST, "vector", after="x_bf110")
        cast_x(1, LAST, "vector", after="x_bf010")
        quantize_x(0, LAST)
        quantize_x(1, LAST)
        x_passes(1, MIDDLE)
        x_passes(0, MIDDLE, last=True)
        q_passes(0, LAST, HIGH_TILES)
        r_passes(0, LAST, HIGH_TILES)
        q_passes(1, LAST, HIGH_TILES)
        r_passes(1, LAST)
        finish(MIDDLE, ("scalar",) * N_TILES, tiles_a_store=2)
        for n in range(N_TILES):
            x_passes(0, LAST, (n,))
            x_passes(1, LAST, (n,), last=True)
        finish(LAST, ("scalar", "vector") * 2, tiles_a_store=1)
